import numpy as np, ml_dtypes
CORES = [13,21,141,149]
N = 4
BF = ml_dtypes.bfloat16
W, NN, NL, P, C, ND, M, RO = 4096, 1024, 512, 192, 32, 4, 4, 6
def look(E, wts, lim, q, D):
    u = (q @ wts) & 4095
    h = (u[:, 0] * u[:, 1]) >> 5
    slot = (h[:, None, None] + 613 * D[:, :, None] + np.arange(M)[None, None, :] * (2 * u[:, 0] + 1)[:, None, None]) & (W - 1)
    slot = slot.reshape(len(q), ND * M)
    dist = np.add.reduce(np.abs(E[slot] - q[:, None, :]), axis=2)
    ok = dist <= lim
    return np.where(np.any(ok, axis=1), slot[np.arange(len(q)), np.argmax(ok, axis=1)], -1), np.min(dist, axis=1)
def wish(NM, K, G):
    rho = np.add.reduce(G, axis=1) & 15
    return (NM[K[np.arange(len(K)), rho]] + G) & 255
def near(x, a, g):
    q = wish(x["NM"][a, g], x["L"][a, g][x["S"][a, g]], x["G"][a, g])
    return look(x["E"][a, g], x["WT"][a, g], 0, q, x["D"][a, g])[1]
def parts(rng):
    def w(hi, *shape): return rng.integers(0, hi, (N, 8) + shape, dtype=np.int32)
    return {"E": w(256, W, 16), "NM": w(256, NN, 16), "L": w(NN, NL, 16), "SG": w(NL, W), "DR": w(256, NL), "WT": w(256, 16, 2), "TH": 850 + w(350), "S": w(NL, P), "D": w(256, P, ND), "G": w(256, P, 16)}
def flat(v):
    return np.ascontiguousarray(v.transpose(0, 1, 3, 2)).reshape(N, 128, v.shape[2])
def tall(v):
    return np.ascontiguousarray(v.astype(np.float32).astype(np.int32).reshape(N, 8, 16, -1).transpose(0, 1, 3, 2))
def pack(x):
    def b(v): return flat(v).astype(np.float32).astype(BF)
    def i(v): return np.ascontiguousarray(v).astype(np.int32)
    return {"ent": b(x["E"]), "nm": b(x["NM"]), "lk": i(flat(x["L"])), "sg": i(x["SG"]), "dr": i(x["DR"]), "wt": i(x["WT"].reshape(N, 128, 2)), "th": i(np.repeat(x["TH"], 16, axis=1).reshape(N, 128, 1)),
            "s0": i(x["S"]), "d0": i(x["D"].transpose(0, 1, 3, 2).reshape(N, 8, ND * P)), "g0": b(x["G"])}
def setup_inputs(rng):
    return pack(parts(rng))
def setup_inputs_room(rng):
    x = parts(rng)
    for a in range(N):
        for g in range(8):
            v = near(x, a, g); lim = np.sort(v)[P // 2 - 1]; A = np.flatnonzero(v <= lim); B = np.flatnonzero(v > lim)
            x["TH"][a, g] = lim
            if len(B) == 0: continue
            n = int(rng.choice(np.array([0, 1, C - 1, C, C + 1, P])))
            if a == 0: n = (C, C + 1, P, C - 1, 1, 0, C, C + 1)[g]
            pick = rng.permutation(np.concatenate([rng.choice(A, P - n), rng.choice(B, n)]))
            for k in ("S", "D", "G"): x[k][a, g] = x[k][a, g][pick]
    return pack(x)
def setup_inputs_ties(rng):
    x = parts(rng)
    for k in ("E", "NM", "G"): x[k] = (x[k] >> 6) << 6
    x["TH"] = (64 * rng.integers(14, 18, (N, 8)) - (np.arange(8) & 1)[None, :]).astype(np.int32)
    r = N - 1
    x["TH"][r] = 4080; x["TH"][r, 5] = 2048; x["TH"][0, 5] = 4080
    for a in (r, 0): x["E"][a, 5] = x["E"][a, 5] & 64
    x["E"][r, 5, :, 0] = 0; x["NM"][r, 5] = 64; x["G"][r, 5] = x["G"][r, 5] & 64; x["G"][r, 5, ::2] = 128
    return pack(x)
def setup_inputs_alike(rng):
    x = parts(rng)
    for k in ("S", "D", "G"): x[k][:, 0] = x[k][:, 0, :1].copy()
    x["E"][:, 1] = x["E"][:, 1, :1].copy()
    x["SG"][:, 2] = rng.choice(np.array([0, NL - 1, 3]), (N, W))
    x["L"][:, 3] = rng.integers(0, NN, (N, 1, 1))
    x["D"][:, 4] = rng.integers(0, 256, (N, 1, 1))
    x["DR"][:, 5] = rng.integers(0, 256, (N, 1))
    x["WT"][:, 6] = 0
    x["E"][:, 7] = np.tile(x["E"][:, 7, :64].copy(), (1, W // 64, 1))
    return pack(x)
def setup_inputs_ends(rng):
    x = parts(rng); who = np.arange(N); even = who % 2 == 0; odd = ~even
    x["TH"][:, 0] = np.where(even, 4080, 0)
    x["NM"][odd, 0] = 0; x["G"][odd, 0, ::2] = 0; x["D"][odd, 0, ::4] = 0; x["L"][even, 0, ::2] = 0
    x["NM"][:, 1] = 0; x["TH"][:, 1] = 0; four = rng.integers(0, 256, (N, 4, 16))
    for a in range(N):
        x["E"][a, 1] = four[a][rng.integers(0, 4, W)]
        close = four[a].copy(); at = rng.integers(0, 16, 4); close[np.arange(4), at] = close[np.arange(4), at] ^ 1
        pool = np.concatenate([four[a], four[(a + 1) % N], close])
        x["G"][a, 1] = pool[rng.permutation(np.arange(P) % 12)]
    x["TH"][:, 2] = np.where(who == 0, 4080, np.where(who == 1, 4079, rng.integers(2000, 4079, N)))
    x["NM"][:, 2] = 0; x["E"][:, 2] = np.where(rng.random((N, W, 1)) < 0.5, 0, x["E"][:, 2]); x["G"][:, 2, ::2] = 255
    x["NM"][:, 3] = 0; x["WT"][:, 3] = 0; x["WT"][:, 3, 0] = 16; x["WT"][:, 3, 1] = 1; x["G"][:, 3, ::2, 0] = 255; x["G"][:, 3, ::2, 1] = 15
    x["L"][:, 4] = rng.choice(np.array([0, NN - 1]), (N, NL, 16)); x["SG"][:, 4] = rng.choice(np.array([0, NL - 1]), (N, W)); x["S"][:, 4] = rng.choice(np.array([0, NL - 1]), (N, P))
    x["DR"][:, 4] = rng.choice(np.array([0, 255]), (N, NL)); x["D"][:, 4] = rng.choice(np.array([0, 255]), (N, P, ND))
    for k in ("E", "NM", "G"): x[k][:, 5] = 255 * (x[k][:, 5] >> 7)
    x["TH"][:, 5] = 1529
    x["WT"][:, 6] = 255; x["NM"][:, 6] = 0; x["TH"][even, 6] = 4080
    x["G"][:, 6, ::2] = rng.integers(225, 256, (N, P // 2, 16)); x["G"][:, 6, 0] = 255
    x["TH"][:, 7] = 0
    return pack(x)
def setup_inputs_spread(rng):
    x = parts(rng)
    def col(n): return (np.exp2(rng.integers(0, 9, (N, 8, n, 1))) * rng.random((N, 8, n, 16))).astype(np.int32) * (rng.random((N, 8, n, 1)) > 0.0625)
    def low(hi, pw, *shape): return np.minimum((hi * rng.random((N, 8) + shape) ** pw).astype(np.int32), hi - 1)
    x["E"] = col(W); x["NM"] = col(NN); x["G"] = col(P)
    x["L"] = low(NN, 3, NL, 16); x["SG"] = low(NL, 2, W); x["DR"] = low(256, 2, NL); x["S"] = low(NL, 2, P); x["D"] = low(256, 3, P, ND)
    x["WT"] = np.minimum(np.exp2(8 * rng.random((N, 8, 16, 2))).astype(np.int32), 255)
    for a in range(N):
        for g in range(8):
            x["TH"][a, g] = np.sort(near(x, a, g))[int(rng.integers(P // 4, 3 * P // 4))]
    return pack(x)
def check_inputs(d):
    bad = []
    for k, hi in (("ent", 255), ("nm", 255), ("lk", NN - 1), ("sg", NL - 1), ("dr", 255), ("wt", 255), ("th", 4080), ("s0", NL - 1), ("d0", 255), ("g0", 255)):
        v = np.asarray(d[k]).astype(np.float64)
        if not (np.min(v) >= 0 and np.max(v) <= hi): bad.append("range of " + k)
        if np.any(v != np.floor(v)): bad.append("whole numbers in " + k)
    t = np.asarray(d["th"]).reshape(N, 8, 16)
    if np.any(t != t[:, :, :1]): bad.append("equal rows of a group in th")
    return bad
def reference(ent, nm, lk, sg, dr, wt, th, s0, d0, g0):
    E = tall(ent); NM = tall(nm); L = np.ascontiguousarray(lk.reshape(N, 8, 16, NL).transpose(0, 1, 3, 2)); WT = wt.astype(np.int32).reshape(N, 8, 16, 2)
    lim = th.reshape(N, 8, 16)[:, :, 0]
    G = tall(g0); D = np.array(d0.reshape(N, 8, ND, P).transpose(0, 1, 3, 2)).astype(np.int32)
    K = np.stack([np.stack([L[a, g][s0[a, g]] for g in range(8)]) for a in range(N)]).astype(np.int32)
    for step in range(RO):
        for a in range(N):
            b = (a + 1) % N
            for g in range(8):
                q = wish(NM[a, g], K[a, g], G[a, g])
                hit = look(E[a, g], WT[a, g], lim[a, g], q, D[a, g])[0]
                own = np.flatnonzero(hit >= 0); miss = np.flatnonzero(hit < 0)[:C]
                far = look(E[b, g], WT[b, g], lim[b, g], q[miss], D[a, g][miss])[0]
                G[a, g] = q
                for who, ix, slot in ((a, own, hit[own]), (b, miss[far >= 0], far[far >= 0])):
                    s = sg[who, g][slot]
                    G[a, g][ix] = E[who, g][slot]
                    K[a, g][ix] = L[who, g][s]
                    D[a, g][ix] = np.concatenate([dr[who, g][s][:, None], D[a, g][ix][:, :ND - 1]], axis=1)
    return {"yk": flat(K).astype(np.float32), "yd": np.ascontiguousarray(D.transpose(0, 1, 3, 2)).reshape(N, 8, ND * P).astype(np.float32), "yg": flat(G).astype(np.float32)}

@@ -1,0 +1,643 @@
+from concourse.mybir import AluOpType, ActivationFunctionType
+
+P, W, NS, STEPS = 192, 224, 4096, 6
+ALU = {"add": AluOpType.add, "sub": AluOpType.subtract, "mul": AluOpType.mult, "max": AluOpType.max, "min": AluOpType.min,
+       "ge": AluOpType.is_ge, "lt": AluOpType.is_lt, "eq": AluOpType.is_equal, "ne": AluOpType.not_equal,
+       "shr": AluOpType.arith_shift_right, "and": AluOpType.bitwise_and}
+ACT = {"id": ActivationFunctionType.Identity, "abs": ActivationFunctionType.Abs, "sign": ActivationFunctionType.Sign,
+       "relu": ActivationFunctionType.Relu}
+SIZE = {"F": 4, "B": 2, "I": 4, "U": 2, "H": 2}
+DTYPE = {"F": "float32", "B": "bfloat16", "I": "int32", "U": "uint16", "H": "float16"}
+CYC, SEM, GAM, PEF, HOP2, HOP2FIRST = 0.00104, 0.08, 1.56, 0.7, 5.5, 8.0
+KINDS0, KINDS, NBACT = "QVAQVA", "QAAQVA", True
+NQY, NQS, SGK = 2, 2, "va"
+VAL = {"0": 0, "1": 1, "2": 2, "4": 4, "9": 9, "a": 20, "b": 50, "c": 120}
+PRIO = ("920ac9219b009410122092c1440acb202c010009094c442290041420a2a24211929902bb440a90a00b1299a20244100b20bc100b00b04a99420ab0094ac01990124224402200200000000104940a900a099a04a42490000a02291290a420a410042221114b902102002499002b4204202000b224422902a220b04ab94040a1212014124100409004442202902909940204b19a0090c44a4902920b9949b0b40400b920a244200090000020000000400001001c042922900200910000010104010000100012010040000a000a0a00a90000000400010002042404410090209b424000400010020020000090014024b410b29b0204a2c42b902c4909102ac9424494090244c4baa04120222210094400baa20900190000042000290c004a0bb91")
+
+
+def cols(v, a, b, step=1):
+    return (v[0], v[1] + a, v[1] + b, step, v[4], v[5], v[6])
+
+
+def rows(v, a, b, step=1):
+    return (v[0], v[1], v[2], v[3], a, b, step)
+
+
+def width(v):
+    return (v[2] - v[1] + v[3] - 1) // v[3]
+
+
+def ind(win, off):
+    return ("ind", win, off)
+
+
+def build():
+    top = {k: 0 for k in SIZE}
+    ops = []
+    marks = []
+
+    def new(kind, n):
+        al = 32 // SIZE[kind]
+        a = top[kind]
+        top[kind] = (a + n + al - 1) // al * al
+        return (kind, a, a + n, 1, 0, 128, 1)
+
+    def bank(i, a, b):
+        return ("P%d" % i, a, b, 1, 0, 128, 1)
+
+    def parts(x):
+        if isinstance(x, tuple):
+            return [x[1], x[2]] if x[0] == "ind" else [x]
+        return []
+
+    def add(eng, kind, args, rd, wr, dur, lat=None):
+        r = [v for x in rd for v in parts(x)]
+        w = []
+        for x in wr:
+            if x[0] == "ind":
+                w.append(x[1]); r.append(x[2])
+            else:
+                w.append(x)
+        ops.append({"eng": eng, "kind": kind, "args": args, "r": r, "w": w, "dur": dur, "lat": dur if lat is None else lat})
+        return len(ops) - 1
+
+    def cost(out, ins, two=False):
+        if out[0] == "ind":
+            return 0.05 + 16 * width(out[2]) * 3.8 * CYC
+        if ins[0][0] == "ind":
+            return 0.06 + width(out) * GAM * CYC
+        n = width(ins[0])
+        if two:
+            n *= 2 if all(x[0][0] != "P" for x in ins) else 1
+        elif SIZE.get(out[0], 4) == 2 and SIZE.get(ins[0][0], 4) == 2:
+            n /= 2
+        return max(64, n) * CYC
+
+    def cp(out, a):
+        return add("v", "cp", (out, a), [a], [out], cost(out, [a]))
+
+    def tt(out, a, b, op):
+        return add("v", "tt", (out, a, b, op), [a, b], [out], cost(out, [a, b], True))
+
+    def ts(out, a, s1, op0, s2=None, op1=None):
+        return add("v", "ts", (out, a, s1, s2, op0, op1), [a, s1, s2], [out], cost(out, [a]))
+
+    def scan(out, a, b, init, op0, op1):
+        return add("v", "scan", (out, a, b, init, op0, op1), [a, b, init], [out], max(64, width(out)) * CYC)
+
+    def mset(out, c):
+        return add("v", "mset", (out, c), [], [out], max(64, width(out) * SIZE[out[0]] / 4) * CYC)
+
+    def act(out, a, f, bias=0.0, scale=1.0, acc=None):
+        d = 0.07 + width(out) * GAM * CYC if a[0] == "ind" else max(64, width(out)) * CYC
+        return add("a", "act", (out, a, f, bias, scale, acc), [a, bias, scale], [out] + ([acc] if acc else []), d)
+
+    def mm(lst, start=True, stop=True):
+        seq = []
+        for i, (o, l, r) in enumerate(lst):
+            first = start and all(x[0] != o for x in lst[:i])
+            last = stop and all(x[0] != o for x in lst[i + 1:])
+            seq.append((o, l, r, first, last))
+        d = sum(max(64, width(r)) * (4 if r[0] == "F" else 1) for o, l, r in lst) * CYC * PEF
+        return add("t", "mm", seq, [x for o, l, r in lst for x in (l, r)], [o for o, l, r in lst], d)
+
+    def iota(out, pat, base, cm):
+        return add("g", "iota", (out, pat, base, cm), [], [out], 0.13 + 2 * width(out) * CYC)
+
+    def asel(out, a, pat, op, fill, base, cm):
+        return add("g", "asel", (out, a, pat, op, fill, base, cm), [a], [out], 0.17 + 2 * width(out) * CYC)
+
+    def load(q, out, name, lat):
+        return add(q, "load", (out, name), [], [out], 0.1, lat)
+
+    def send(name, src, dst, nxt, lat):
+        i = add("g", "send", (name, src, dst, nxt), [src], [], 0.4)
+        j = add(None, "recv", (name,), [], [dst], 0.0, 0.0)
+        ops[j]["after"] = (i, lat)
+
+    ENT = new("B", W + NS); QB = cols(ENT, 0, W); TAB = cols(ENT, W, W + NS)
+    NM = new("B", 1024); GB = new("B", P); DK = new("B", W); DRZ = new("B", W + 512); OK = new("B", W)
+    SG = new("F", W + NS); SGT = cols(SG, W, W + NS)
+    KW = new("F", W + 512); KB = cols(KW, 0, W); LS = new("F", W + 512); NF = new("F", W); KN = new("F", P)
+    SL = new("I", 2 * W); SLO = cols(SL, 0, W); SLN = cols(SL, W, 2 * W)
+    wtI = new("I", 2); wnI = new("I", 2); thI = new("I", 1)
+    s0I = rows(new("I", P), 0, 8); d0I = rows(new("I", P), 0, 32); drI = rows(new("I", 512), 0, 8)
+    sgI = rows(new("I", 1024), 0, 32); lkI = new("I", 512)
+    asko = [new("F", 64) for s in range(STEPS)]; aski = [new("F", 64) for s in range(STEPS)]
+    rpo = [new("H", 96) for s in range(STEPS)]; rpi = [new("H", 96) for s in range(STEPS)]
+
+    load("s", wtI, "wt", 2.2); load("a", s0I, "s0", 2.2); load("s", GB, "g0", 2.4); load("a", lkI, "lk", 3.0)
+    load("s", d0I, "d0", 2.4); load("a", NM, "nm", 3.6); load("s", thI, "th", 2.4)
+    load("a", sgI, "sg", 4.0); load("a", drI, "dr", 4.0); load("s", TAB, "ent", 8.0)
+    send("mw", wtI, wnI, False, HOP2FIRST)
+
+    rowI = new("I", 1); iota(rowI, [[0, 1]], 0, 1)
+    CA = new("B", 256); iota(CA, [[0, 16], [1, 16]], 0, 0)
+    CG = new("B", 256); iota(CG, [[1, 16], [0, 16]], 0, 0)
+    COL = new("B", W); iota(COL, [[1, W]], 0, 0)
+    MC = new("B", 128); iota(MC, [[0, 32], [-1, 4]], 3, 0)
+    S32 = new("B", 128); iota(S32, [[4, 8], [-1, 4], [0, 4]], 3, 0)
+    POS = new("F", 512); iota(POS, [[1, 512]], 32, 0)
+    tI = new("I", 2); rowf = new("F", 1); rowa = new("F", 1); rowg = new("F", 1)
+    cp(rowf, rowI)
+    ts(cols(tI, 0, 1), rowI, 15, "and"); cp(rowa, cols(tI, 0, 1))
+    ts(cols(tI, 1, 2), rowI, 4, "shr"); cp(rowg, cols(tI, 1, 2))
+    c128 = lambda v: cols(v, 0, 128)
+    MK = new("B", 256); ts(MK, CA, rowa, "eq")
+    ML = rows(c128(MK), 0, 16)
+    MR = rows(new("B", P), 0, 16); ts(MR, rows(cols(MK, 0, P), 0, 16), -1.0, "add", 32768.0, "mul")
+    RS0 = new("B", 256); ts(RS0, CA, 0.0, "ne")
+    SEL8 = rows(new("H", 128), 0, 8); ts(SEL8, rows(c128(CG), 0, 8), rows(rowf, 0, 8), "eq")
+    Bm = new("B", 128); ts(Bm, c128(CG), rowg, "eq")
+    Bh = new("H", 128); ts(Bh, c128(CG), rowg, "eq")
+    B16 = new("B", 128); ts(B16, c128(CG), rowg, "eq", 0.0625, "mul")
+    B16h = new("H", 128); ts(B16h, c128(CG), rowg, "eq", 0.0625, "mul")
+    Bf = new("F", 128); ts(Bf, c128(CG), rowg, "eq")
+    B224 = new("B", 128); ts(B224, c128(CG), rowg, "eq", float(W), "mul")
+    BP = new("B", 128); ts(BP, c128(CG), rowg, "eq", 1024.0, "mul")
+    BN = new("B", 128); ts(BN, c128(CG), rowg, "eq", -1024.0, "mul")
+    ONE = new("B", 256); mset(ONE, 1.0)
+    ONEF = new("F", W); mset(ONEF, 1.0)
+    NI = rows(new("B", 128), 0, 1); ts(NI, rows(c128(CA), 0, 1), -0.0625, "mul")
+    MROW = rows(new("B", 128), 0, 1); cp(MROW, rows(MC, 0, 1))
+    I608 = new("B", 128); ts(I608, c128(COL), rowf, "eq", 608.0, "mul")
+    I5 = new("B", 128); ts(I5, c128(COL), rowf, "eq", 5.0, "mul")
+    SEL32 = rows(new("H", 128), 0, 32); ts(SEL32, rows(S32, 0, 32), rows(rowf, 0, 32), "eq")
+    tA = new("B", 128); tB = new("B", 128); MA = new("B", 128); MB = new("B", 128)
+    ts(tA, MC, 2.0, "mul", 4.0, "min"); tt(MA, tA, Bm, "mul")
+    ts(tB, MC, 3.0, "eq", 2.0, "mul"); tt(MB, tB, Bm, "mul")
+    REPO = new("U", P); ts(REPO, cols(POS, 0, P), -32.0, "add")
+    ucol = new("F", 1); ts(ucol, rowg, 16.0, "mul", 15.0, "add")
+    UM = new("B", 144); ts(UM, cols(COL, 0, 144), ucol, "eq")
+    thF = new("F", 1); thp = new("F", 1); pt0 = new("F", 1); pt1 = new("F", 1); PT = new("B", 256)
+    cp(thF, thI); ts(thp, thF, 0.5, "add")
+    ts(pt0, rowa, -256.0, "mul", thF, "add"); ts(pt1, pt0, 1.0, "add", 0.0, "max")
+    ts(PT, ONE, pt1, "mul", 256.0, "min")
+    MR2 = rows(new("B", 256), 0, 16); ts(MR2, rows(CG, 0, 16), rows(rowf, 0, 16), "ne", -8388608.0, "mul")
+    PW = new("F", 12); ts(PW, cols(COL, 0, 12), 16.0, "mul", rowa, "add")
+    JB = new("F", 2); ts(JB, cols(PW, 0, 2), 0.5, "add")
+    Id = new("B", 128); ts(Id, c128(COL), rowf, "eq")
+    NID = new("B", 128); ts(NID, c128(COL), rowf, "eq", -1.0, "mul")
+    tI3 = new("I", 1); row32 = new("F", 1); RR = new("B", 512)
+    ts(tI3, rowI, 31, "and"); cp(row32, tI3)
+    ts(cols(RR, 0, 256), CG, row32, "eq"); ts(cols(RR, 256, 512), CG, row32, "sub", -16.0, "eq")
+    tC = new("B", 128); TRI = new("B", 128)
+    asel(tC, Bm, [[-1, 128]], "ge", 0.0, 0, 1); asel(TRI, tC, [[-1, 128]], "ne", -1.0, 0, 1)
+    tbias = new("F", 1); ts(tbias, rowa, 0.5, "mul", -7.0, "add")
+    tF = new("B", 128); DM = new("B", 128)
+    asel(tF, Bm, [[-1, 128]], "eq", 0.0, -4, 1); asel(DM, tF, [[-1, 128]], "ne", -1.0, 0, 1)
+    VC = new("F", W); ts(VC, COL, float(P), "lt", -1.0, "mul")
+    tG = rows(new("B", 128), 0, 8); SELD = rows(new("H", 128), 0, 8)
+    ts(tG, rows(c128(CA), 0, 8), 12.0, "ge"); tt(SELD, tG, SEL8, "mul")
+    tH = rows(new("B", 128), 0, 32); ts(tH, rows(c128(CG), 0, 32), 4.0, "mul", rows(rowf, 0, 32), "sub")
+    SELS = [rows(new("H", 128), 0, 32) for c in range(4)]
+    for c in range(4):
+        ts(SELS[c], tH, float(-c), "eq")
+    WM = {}; WS = {}
+    for nm_, src, base, step in (("o", wtI, 7, -1), ("n", wnI, -8, 1)):
+        wf = new("F", 2); cp(wf, src)
+        m4 = [new("B", 128) for k in range(4)]
+        for k, (mat, c) in enumerate(((Bm, 0), (Bm, 1), (MA, 0), (MB, 0))):
+            ts(m4[k], mat, cols(wf, c, c + 1), "mul")
+        WM[nm_] = m4
+        part = new("B", 128); asel(part, Bm, [[0, 8], [step, 16]], "ge", 0.0, base, 0)
+        WS[nm_] = [new("B", 128) for j in range(2)]
+        for j in range(2):
+            ts(WS[nm_][j], part, cols(wf, j, j + 1), "mul")
+    SLOW = new("H", 128); SHIGH = new("H", 128); r0 = new("F", 1); r8 = new("F", 1)
+    ts(r0, rowa, 0.0, "eq"); ts(r8, rowa, 8.0, "eq"); ts(SLOW, Bm, r0, "mul"); ts(SHIGH, Bm, r8, "mul")
+    MROW2 = rows(new("B", 128), 0, 2); tY = rows(new("F", 128), 0, 2)
+    ts(tY, rows(MC, 0, 2), -1.0, "mul", 2048.0, "add")
+    ts(tY, tY, rows(rowf, 0, 2), "mul"); tt(MROW2, tY, rows(MC, 0, 2), "add")
+    mset(cols(QB, P, W), 0.0); mset(cols(DK, P, W), 0.0); mset(cols(OK, P, W), -1.0); mset(cols(NF, P, W), 0.0)
+    mset(cols(KB, P, W), 0.0); mset(cols(SLO, P, W), 0); mset(cols(SLN, P, W), 0)
+    mset(cols(DRZ, 0, W), 0.0); mset(cols(LS, 0, W), 0.0); cp(cols(SG, 0, W), COL)
+    DW = new("B", 544); SW = new("F", 544); mset(cols(DW, 0, 32), 0.0); mset(cols(SW, 0, 32), 0.0)
+
+    cp(cols(KW, W, W + 512), lkI)
+    sc_b = new("F", P); s0h = rows(new("H", P), 0, 8); off0 = new("U", 12)
+    cp(s0h, s0I)
+    pb = bank(4, 0, P)
+    mm([(pb, ML, MR)], stop=False); mm([(pb, SEL8, s0h)], start=False)
+    scan(sc_b, cols(RS0, 0, P), pb, 0.0, "mul", "max"); cp(off0, cols(sc_b, 15, P, 16))
+    cp(KN, ind(cols(KW, W, W + 512), off0))
+    d0h = rows(new("H", P), 0, 32); cp(d0h, d0I)
+    mm([(bank(5, 0, P), SEL32, d0h)]); act(cols(DK, 0, P), bank(5, 0, P), "id")
+
+    def tables():
+        act(cols(LS, W, W + 512), cols(KW, W, W + 512), "id", 1024.0)
+        drh = rows(new("H", 512), 0, 8); cp(drh, drI)
+        mm([(bank(2, 0, 512), SELD, drh)]); act(cols(DRZ, W, W + 512), bank(2, 0, 512), "id")
+        sgh = rows(new("H", 1024), 0, 32)
+        for h in range(2):
+            cp(cols(sgh, 512 * h, 512 * h + 512), cols(sgI, 512 * h, 512 * h + 512))
+        for k in range(8):
+            pk = bank(2 + (k + 1) % 2, 0, 512)
+            mm([(pk, SELS[k // 2], cols(sgh, 512 * (k % 2), 512 * (k % 2) + 512))])
+            act(cols(SGT, 512 * k, 512 * k + 512), pk, "id", float(W))
+
+    def scratch(n, nh):
+        return {"r": new("I", n), "x": new("H", n), "sc": new("F", n), "co": new("U", max(2, n // 16)),
+                "xs": new("F", n), "u": new("I", 2 * nh), "u2": new("I", 2 * nh), "h": new("I", nh), "h2": new("I", nh)}
+
+    def wish(S, n, G, K, q, p1, p2, half):
+        y = bank(p1, 0, n); c = bank(p2, 0, n)
+        mm([(y, NI, rows(cols(ONE, 0, n), 0, 1))], stop=False); mm([(y, B16h if half else B16, G)], start=False)
+        cp(S["r"], y); tt(y, S["r"], y, "eq"); tt(S["x"], K, y, "mul")
+        mm([(c, ML, cols(MR, 0, n))], stop=False); mm([(c, Bh, S["x"])], start=False)
+        scan(S["sc"], cols(RS0, 0, n), c, 0.0, "mul", "max"); cp(S["co"], cols(S["sc"], 15, n, 16))
+        tt(S["xs"], ind(NM, S["co"]), G, "add")
+        ts(y, S["xs"], 256.0, "ge", -256.0, "mul"); tt(q, S["xs"], y, "add")
+
+    def slots(S, n, q, D, who, out, pu, pl):
+        m = n * len(who)
+        for k, w in enumerate(who):
+            o = bank(pl, k * n, k * n + n)
+            mm([(o, MROW, rows(cols(ONE, 0, n), 0, 1)), (o, I608, D), (o, I5, D)], stop=False)
+            if k == 0:
+                mm([(bank(pu, (j * len(who) + kk) * n, (j * len(who) + kk + 1) * n), WM[ww][j], q)
+                    for j in range(2) for kk, ww in enumerate(who)])
+            mm([(o, WM[w][2], q), (o, WM[w][3], q)], start=False)
+        u, u2, h, h2 = cols(S["u"], 0, 2 * m), cols(S["u2"], 0, 2 * m), cols(S["h"], 0, m), cols(S["h2"], 0, m)
+        cp(u, bank(pu, 0, 2 * m)); ts(u2, u, 4095, "and")
+        tt(h, cols(u2, 0, m), cols(u2, m, 2 * m), "mul"); ts(h2, h, 5, "shr")
+        tt(h, h2, bank(pl, 0, m), "add"); ts(out, h, 4095, "and")
+
+    H = P // 2
+    SB = [scratch(H, H) for h in range(2)]; SN = [scratch(16, H) for h in range(2)]; SY = scratch(32, 64)
+    offB = new("U", P); QR = new("B", 16 * P); DF = new("B", 16 * P)
+    QT = rows(new("B", 256), 0, 96); hh = new("H", P)
+
+    def slots_both(h, q, D, bx, by):
+        one = rows(cols(ONE, 0, H), 0, 2); S = SB[h]; hq = cols(hh, H * h, H * h + H)
+        lin = lambda o, w: [(o, MROW2, one), (o, I608, D), (o, I5, D), (o, w[2], q), (o, w[3], q)]
+        mm([(bank(bx, j * H, j * H + H), WS[w][j], q) for j in range(2) for w in "on"])
+        o = bank(by, 0, H); o2 = bank(bx, 0, H)
+        mm(lin(o, WM["o"]), stop=False)
+        cp(S["u"], bank(bx, 0, 2 * H)); ts(S["u2"], S["u"], 4095, "and")
+        mm(lin(o2, WM["n"]), stop=False)
+        tt(S["h"], cols(S["u2"], 0, H), cols(S["u2"], H, 2 * H), "mul")
+        ts(S["h2"], S["h"], 5, "shr", 4095, "and"); ts(hq, S["h2"], -2048.0, "add")
+        mm([(o, SLOW, hq)], start=False); mm([(o2, SHIGH, hq)], start=False)
+        cp(S["h"], o); ts(cols(SLO, H * h, H * h + H), S["h"], 4095, "and")
+        cp(SN[h]["h"], o2); ts(cols(SLN, H * h, H * h + H), SN[h]["h"], 4095, "and")
+
+    def big_look(h, kinds, both):
+        a0, a1 = H * h, H * h + H
+        half = lambda v: cols(v, a0, a1)
+        bx, by = 4 + 2 * h, 5 + 2 * h
+        q = half(QB); D = half(DK)
+        wish(SB[h], H, half(GB), half(KN), q, bx, by, False)
+        act(half(KB), half(KN), "id")
+        if kinds[3 * h:3 * h + 3] != "QQQ":
+            mm([(rows(bank(by, 0, 128), 0, 96), q, NID)])
+            act(cols(QT, 128 * h, 128 * h + 128), rows(bank(by, 0, 128), 0, 96), "id")
+        if both:
+            slots_both(h, q, D, bx, by)
+        else:
+            slots(SB[h], H, q, D, "o", half(SLO), bx, by)
+        cp(half(offB), half(SLO))
+        for c in range(3 * h, 3 * h + 3):
+            if kinds[c] == "Q":
+                for a in (32 * c, 32 * c + 16):
+                    x, y = 16 * a, 16 * a + 256
+                    act(cols(QR, x, y), ind(q, cols(REPO, a - a0, a - a0 + 16)), "id")
+                    tt(cols(DF, x, y), ind(TAB, cols(offB, a, a + 16)), cols(QR, x, y), "sub")
+                    act(cols(DF, x, y), cols(DF, x, y), "abs")
+            else:
+                o = bank(by, 0, 512); j = 32 * (c % 3); eg = cols(QR, 512 * c, 512 * c + 512)
+                for a in (0, 16):
+                    src = ind(TAB, cols(offB, 32 * c + a, 32 * c + a + 16)); dst = cols(eg, 16 * a, 16 * a + 256)
+                    act(dst, src, "id") if kinds[c] == "A" else cp(dst, src)
+                mm([(o, rows(cols(QT, 128 * h, 128 * h + 128), j, j + 32), rows(RR, j, j + 32))], stop=False)
+                mm([(o, Id, eg)], start=False)
+                act(cols(DF, 512 * c, 512 * c + 512), o, "abs")
+        if not both:
+            slots(SN[h], H, q, D, "n", half(SLN), bx, by)
+        o = bank(bx, 0, H)
+        mm([(o, cols(UM, 15 - r, 143 - r), cols(DF, 16 * a0 + r, 16 * a1, 16)) for r in range(16)])
+        act(half(OK), o, "sign", thp, -1.0)
+        mm([(o, Bm, half(OK))]); act(half(NF), o, "sign", -16.0, -1.0)
+
+    first = new("B", P); fs = new("F", P); sm = new("F", P); dtm = new("B", P); dts = new("B", P)
+    mx = [new("F", 6) for h in range(2)]; offG = [new("U", 6) for h in range(2)]; offS = [new("U", 6) for h in range(2)]
+
+    def big_update(h):
+        half = lambda v: cols(v, H * h, H * h + H)
+        x, o = bank(4 + 2 * h, 0, H), bank(5 + 2 * h, 0, H)
+        sc = half(sc_b); last = cols(sc, 15, H, 16)
+        mm([(x, TRI, half(OK))]); act(half(first), x, "relu", tbias, -0.5)
+        act(x, x, "relu", tbias, -0.5)
+        tt(half(fs), half(SLO), x, "mul")
+        mm([(o, ML, cols(MR, 0, H)), (o, B224, half(first))], stop=False); mm([(o, Bf, half(fs))], start=False)
+        scan(sc, cols(RS0, 0, H), o, 0.0, "mul", "max")
+        tt(mx[h], last, cols(PW, 6 * h, 6 * h + 6), "max"); cp(offG[h], mx[h])
+        tt(half(sm), ind(SG, offG[h]), cols(MK, 0, H), "mul")
+        act(half(GB), ind(ENT, offG[h]), "id")
+        scan(sc, cols(RS0, 0, H), half(sm), 0.0, "mul", "max"); cp(offS[h], last)
+        act(half(KN), ind(KW, offS[h]), "id")
+        mm([(x, DM, half(DK))]); tt(half(dtm), x, half(NF), "mul")
+        act(half(dts), ind(DRZ, offS[h]), "id")
+        mm([(x, Id, half(DK)), (x, NID, half(dtm))], stop=False); mm([(x, Id, half(dts))], start=False); act(half(DK), x, "id")
+
+    kold = new("F", 32); dold = new("B", 32); dlt = new("B", 32); vy = new("F", 32)
+    f1 = new("F", 32); kt = new("F", 32); ky = new("F", 32); dy1 = new("F", 32); dyt = new("F", 32); dy = new("B", 32)
+    qy = new("B", 32); sly = new("I", 64); offY = new("U", 32); oky = new("B", 32)
+    QS = new("B", 512); AS = new("B", 512); st = new("F", 512); DY = new("B", 512)
+    cnt = new("F", W); junk = [new("B", W) for b in range(2)]; acc = new("F", 2)
+    lst = [new("U", 2) for s in range(STEPS)]
+
+    def merge(s):
+        G, Kp, Z = (cols(rpi[s], 32 * k, 32 * k + 32) for k in range(3))
+        ts(f1, Kp, 1024.0, "ge", 1024.0, "mul"); tt(kt, Kp, kold, "max")
+        tt(dy1, Z, dold, "add"); tt(dyt, f1, dlt, "mul")
+        return G
+
+    def small_look(s):
+        L = lst[s - 1]
+        G = merge(s - 1)
+        tt(ky, kt, f1, "sub"); tt(dy, dy1, dyt, "add")
+        wish(SY, 32, G, ky, qy, 2, 3, True)
+        slots(SY, 32, qy, dy, "on", sly, 2, 3)
+        cp(offY, cols(sly, 0, 32))
+        n = 32 // NQY
+        for b in range(NQY):
+            x, y = 16 * n * b, 16 * n * (b + 1)
+            o = bank(b % 2, 0, y - x)
+            act(cols(QS, x, y), ind(qy, cols(REPO, n * b, n * b + n)), "id")
+            tt(cols(DY, x, y), ind(TAB, cols(offY, n * b, n * b + n)), cols(QS, x, y), "sub")
+            act(cols(AS, x, y), cols(DY, x, y), "abs")
+            mm([(o, BN, cols(PT, 0, y - x))], stop=False); mm([(o, BP, cols(AS, x, y))], start=False)
+            scan(cols(st, x, y), cols(RS0, 0, y - x), o, 0.0, "mul", "min")
+        tt(ind(NF, L), cols(st, 15, 512, 16), vy, "max")
+        cp(ind(QB, L), qy); cp(ind(SLN, L), cols(sly, 32, 64))
+        o = bank(2, 0, 32)
+        mm([(o, cols(UM, 15 - r, 143 - r), cols(AS, r, 512, 16)) for r in range(16)])
+        act(oky, o, "sign", thp, -1.0)
+        cp(ind(OK, L), oky); cp(ind(SLO, L), cols(sly, 0, 32)); cp(ind(KB, L), ky); cp(ind(DK, L), dy)
+
+    def ask(s):
+        scan(cnt, NF, ONEF, 0.0, "add", "add")
+        for b in range(2):
+            act(junk[b], cnt, "sign", cols(JB, b, b + 1), -1.0, cols(acc, b, b + 1))
+        ts(lst[s], acc, 0.5, "mul", W / 2.0, "add")
+        cp(cols(asko[s], 32, 64), ind(SLN, lst[s]))
+        act(cols(asko[s], 0, 32), ind(QB, lst[s]), "id")
+        send("ma%d" % s, asko[s], aski[s], True, HOP2)
+        act(kold, ind(KB, lst[s]), "id"); act(dold, ind(DK, lst[s]), "id"); act(vy, ind(VC, lst[s]), "id")
+        mm([(bank(3, 0, 32), DM, dold)]); act(dlt, bank(3, 0, 32), "id", 0.0, 1.0 / 1024)
+
+    so = new("U", 32); idx = new("U", 2); sm2 = new("F", 32); sc2 = new("F", 32); of2 = new("U", 2)
+
+    def serve(s):
+        q = cols(aski[s], 0, 32)
+        cp(so, cols(aski[s], 32, 64))
+        n = 32 // NQS
+        for b in range(NQS):
+            x, y = 16 * n * b, 16 * n * (b + 1)
+            o = bank(b % 2, 0, y - x)
+            act(cols(QS, x, y), ind(q, cols(REPO, n * b, n * b + n)), "id")
+            tt(cols(DW, 32 + x, 32 + y), ind(TAB, cols(so, n * b, n * b + n)), cols(QS, x, y), "sub")
+            act(cols(AS, x, y), cols(DW, 32 + x, 32 + y), "abs")
+            mm([(o, BP, cols(PT, 0, y - x)), (o, ML, cols(MR2, x % 256, x % 256 + y - x))], stop=False)
+            mm([(o, BN, cols(AS, x, y))], start=False)
+            scan(cols(st, x, y), o, cols(POS, x, y), cols(st, x - 1, x) if x % 256 else cols(PW, x // 256, x // 256 + 1), "max", "min")
+        for b in range(2):
+            dst, src = cols(SW, 32 + 256 * b, 288 + 256 * b), ind(SGT, cols(so, 16 * b, 16 * b + 16))
+            cp(dst, src) if SGK[b] == "v" else act(dst, src, "id")
+        cp(idx, cols(st, 255, 512, 256))
+        tt(sm2, ind(SW, idx), cols(MK, 0, 32), "mul")
+        tt(cols(rpo[s], 0, 32), ind(DW, idx), q, "add")
+        scan(sc2, cols(RS0, 0, 32), sm2, 0.0, "mul", "max"); cp(of2, cols(sc2, 15, 32, 16))
+        cp(cols(rpo[s], 32, 64), ind(LS, of2)); cp(cols(rpo[s], 64, 96), ind(DRZ, of2))
+        send("mr%d" % s, rpo[s], rpi[s], False, HOP2)
+
+    for s in range(STEPS):
+        marks.append(len(ops))
+        for h in range(2):
+            big_look(h, KINDS if s else KINDS0, NBACT and s > 0)
+        if s:
+            small_look(s)
+        ask(s)
+        if s == 0:
+            tables()
+        serve(s)
+        big_update(0); big_update(1)
+    marks.append(len(ops))
+    OG = new("F", W); OD = new("F", W); L = lst[STEPS - 1]
+    mset(cols(OG, P, W), 0.0); mset(cols(OD, P, W), 0.0)
+    act(cols(KB, 0, P), KN, "id"); act(cols(OG, 0, P), GB, "id"); act(cols(OD, 0, P), cols(DK, 0, P), "id")
+    G = merge(STEPS - 1)
+    cp(ind(OG, L), G); tt(ind(KB, L), kt, f1, "sub"); tt(ind(OD, L), dy1, dyt, "add")
+
+    def store(q, name, a, src):
+        add(q, "store", (name, a, src), [src], [], 0.1, 2.2)
+    store("s", "yg", None, cols(OG, 0, P)); store("a", "yk", None, cols(KB, 0, P))
+    for d in range(4):
+        store("sa"[d % 2], "yd", d, rows(cols(OD, 0, P), 12 - 4 * d, 128, 16))
+    per = marks[2] - marks[1]
+    for i, o in enumerate(ops):
+        o["role"] = i if i < marks[2] else (marks[1] + (i - marks[1]) % per if i < marks[-1] else marks[2] + i - marks[-1])
+    return ops, top
+
+
+def depend(ops):
+    hist = {}
+    for i, o in enumerate(ops):
+        d = set()
+        spans = []
+        for v, wr in [(v, False) for v in o["r"]] + [(v, True) for v in o["w"]]:
+            spans.append((v[0], 0, 1, True) if v[0][0] == "P" else (v[0], v[1], v[2], wr))
+        for b, x, y, wr in spans:
+            for (x2, y2, wr2, j) in hist.get(b, []):
+                if x < y2 and x2 < y and (wr or wr2):
+                    d.add(j)
+        for b, x, y, wr in spans:
+            h = hist.setdefault(b, [])
+            if wr:
+                h[:] = [e for e in h if not (x <= e[0] and e[1] <= y)]
+            h.append((x, y, wr, i))
+        d.discard(i)
+        o["deps"] = d
+
+
+def schedule(ops, wts=None):
+    n = len(ops)
+    dur = [o["dur"] for o in ops]
+    succ = [[] for i in range(n)]
+    for i, o in enumerate(ops):
+        es = [(j, ops[j]["lat"] + (0.0 if ops[j]["eng"] is None or ops[j]["eng"] == o["eng"] == "t" else SEM)) for j in o["deps"]]
+        if "after" in o:
+            es.append(o["after"])
+        for j, e in es:
+            succ[j].append((i, e))
+    lvl = [0.0] * n
+    for i in range(n - 1, -1, -1):
+        lvl[i] = max([ops[i]["lat"]] + [e + lvl[k] for k, e in succ[i]]) + 1e-6 + (0.1 * wts[ops[i]["role"]] if wts else 0.0)
+    busy = {}
+    ready = [0.0] * n
+    for i in sorted(range(n), key=lambda i: (-lvl[i], i)):
+        t = ready[i]
+        if ops[i]["eng"] is not None:
+            line = busy.setdefault(ops[i]["eng"], [])
+            k = len(line)
+            while k > 0 and line[k - 1][1] > t:
+                k -= 1
+            while k < len(line) and t + dur[i] > line[k][0]:
+                t = max(t, line[k][1])
+                k += 1
+            line.insert(k, (t, t + dur[i]))
+        ops[i]["t"] = t
+        for k2, e in succ[i]:
+            ready[k2] = max(ready[k2], t + e + 1e-6)
+    return sorted(range(n), key=lambda i: (ops[i]["t"], i))
+
+
+def syncs(ops, order):
+    pos = {}
+    known = {}
+    for i in order:
+        o = ops[i]
+        e = o["eng"]
+        own = o["kind"] in ("load", "store", "recv")
+        o["lane"] = ("x", i) if own else e
+        pos[e] = pos.get(e, 0) + 1
+        o["pos"] = 1 if own else pos[e]
+        o["waits"] = []
+        if e is None:
+            o["clock"] = {o["lane"]: 1}
+            continue
+        k = known.setdefault(e, {})
+        for j in sorted(o["deps"], key=lambda j: -ops[j]["t"]):
+            pj = ops[j]
+            if pj["kind"] == "send" or (pj["eng"] == "t" and e == "t"):
+                continue
+            if k.get(pj["lane"], 0) >= pj["pos"]:
+                continue
+            o["waits"].append(j)
+            pj["sig"] = True
+            for l, c in pj["clock"].items():
+                if k.get(l, 0) < c:
+                    k[l] = c
+        c = dict(k)
+        c[o["lane"]] = o["pos"]
+        o["clock"] = c
+    cnt = {}
+    for i in order:
+        o = ops[i]
+        if o["kind"] in ("load", "store"):
+            o["sem"] = ("d%d" % len([1 for x in cnt if x[0] == "d"]), 16)
+            cnt[o["sem"][0]] = 16
+        elif o["kind"] == "recv":
+            o["sem"] = (o["args"][0], None)
+        elif o.get("sig"):
+            nm_ = "q" + o["eng"]
+            cnt[nm_] = cnt.get(nm_, 0) + 1
+            o["sem"] = (nm_, cnt[nm_])
+    return cnt
+
+
+OPS, TOP = build()
+depend(OPS)
+ORDER = schedule(OPS, [VAL[c] for c in PRIO])
+FINAL = syncs(OPS, ORDER)
+MSGS = [OPS[i]["args"] for i in ORDER if OPS[i]["kind"] == "send"]
+
+SCRATCH = {"sb" + k: ("sbuf", [128, TOP[k]], DTYPE[k]) for k in SIZE}
+SCRATCH.update({"ps%d" % i: ("psum", [128, 512], "float32") for i in range(8)})
+SEMAPHORES = sorted(FINAL) + [m[0] for m in MSGS] + ["sent"]
+
+
+def count(mask):
+    return bin(mask).count("1")
+
+
+def relay_of(T, topo, rank):
+    n = len(T.cores)
+    c = T.cores[rank]
+    ok = [x for x in topo.cores_of(c) if x not in T.cores and topo.may_write(x, T.cores[(rank + 1) % n])
+          and topo.may_write(x, T.cores[(rank - 1) % n])]
+    return sorted(ok, key=lambda x: topo.die(x) != topo.die(c))[0]
+
+
+def rank_program(g, core, T, topo):
+    n = len(T.cores)
+
+    def ap(v):
+        if not isinstance(v, tuple):
+            return v
+        if v[0] == "ind":
+            return ap(v[1]).indirect(ap(v[2]))
+        t = T["ps" + v[0][1:]] if v[0][0] == "P" else T["sb" + v[0]]
+        if v[6] != 1:
+            return t[v[4]:v[5]:v[6], v[1]:v[2]]
+        if v[3] != 1:
+            return t[v[4]:v[5], v[1]:v[2]:v[3]]
+        return t[v[4]:v[5], v[1]:v[2]]
+
+    rank = T.rank_of(core)
+    if rank is None:
+        for r in range(n):
+            if relay_of(T, topo, r) != core:
+                continue
+            total = 0
+            for name, src, dst, nxt in MSGS:
+                to = T.cores[(r + (1 if nxt else -1)) % n]
+                rid, pid = topo.addr(to, core)
+                m = topo.mask(core, to)
+                g.wait_ge(T.sem[name], count(topo.mask(T.cores[r], core)))
+                g.remote_dma(ap(dst), ap(dst), T.sem[name], T.sem.sent, pid, rid, m)
+                total += count(m)
+            g.wait_ge(T.sem.sent, total)
+        return
+    relay = relay_of(T, topo, rank)
+    rid, pid = topo.addr(relay, core)
+    m1 = topo.mask(core, relay)
+    got = {}
+    for name, src, dst, nxt in MSGS:
+        got[name] = count(topo.mask(relay_of(T, topo, (rank + (-1 if nxt else 1)) % n), core))
+    Q = {"g": g, "v": g.vector, "a": g.scalar, "t": g.tensor, "s": g.sync}
+    for i in ORDER:
+        o = OPS[i]
+        k, a = o["kind"], o["args"]
+        if k == "recv":
+            continue
+        q = Q[o["eng"]]
+        for j in o["waits"]:
+            s, c = OPS[j]["sem"]
+            q.wait_ge(T.sem[s], got[s] if c is None else c)
+        if k == "send":
+            g.remote_dma(ap(a[2]), ap(a[1]), T.sem[a[0]], T.sem.sent, pid, rid, m1)
+            continue
+        if k == "cp":
+            x = q.tensor_copy(ap(a[0]), ap(a[1]))
+        elif k == "tt":
+            x = q.tensor_tensor(ap(a[0]), ap(a[1]), ap(a[2]), ALU[a[3]])
+        elif k == "ts":
+            if a[5] is None:
+                x = q.tensor_scalar(ap(a[0]), ap(a[1]), ap(a[2]), None, ALU[a[4]])
+            else:
+                x = q.tensor_scalar(ap(a[0]), ap(a[1]), ap(a[2]), ap(a[3]), ALU[a[4]], ALU[a[5]])
+        elif k == "scan":
+            x = q.tensor_tensor_scan(ap(a[0]), ap(a[1]), ap(a[2]), ap(a[3]), ALU[a[4]], ALU[a[5]])
+        elif k == "mset":
+            x = q.memset(ap(a[0]), a[1])
+        elif k == "act":
+            x = q.activation(ap(a[0]), ap(a[1]), ACT[a[2]], bias=ap(a[3]), scale=ap(a[4]), accum_out=ap(a[5]))
+        elif k == "mm":
+            for (out, l, r, st, sp) in a:
+                x = q.matmul(ap(out), ap(l), ap(r), st, sp)
+        elif k == "iota":
+            x = g.iota(ap(a[0]), a[1], a[2], a[3], allow_small_or_imprecise_dtypes=True)
+        elif k == "asel":
+            x = g.affine_select(ap(a[0]), ap(a[1]), a[2], ALU[a[3]], a[4], a[5], a[6])
+        elif k == "load":
+            x = q.dma_start(ap(a[0]), T[a[1]][:])
+        elif k == "store":
+            dst = T[a[0]][:] if a[1] is None else T[a[0]][:, a[1] * P:(a[1] + 1) * P]
+            x = q.dma_start(dst, ap(a[2]))
+        if "sem" in o:
+            x.then_inc(T.sem[o["sem"][0]], 16 if k in ("load", "store") else 1)
+    for s in sorted(FINAL):
+        g.wait_ge(T.sem[s], FINAL[s])
+    g.wait_ge(T.sem.sent, len(MSGS) * count(m1))

@@ -8,11 +8,11 @@ ACT = {"id": ActivationFunctionType.Identity, "abs": ActivationFunctionType.Abs,
        "relu": ActivationFunctionType.Relu}
 SIZE = {"F": 4, "B": 2, "I": 4, "U": 2, "H": 2}
 DTYPE = {"F": "float32", "B": "bfloat16", "I": "int32", "U": "uint16", "H": "float16"}
-CYC, SEM, GAM, PEF, HOP2, HOP2FIRST = 0.00104, 0.08, 1.56, 0.7, 5.5, 8.0
+CYC, SEM, GAM, PEF, HOP2, HOP2FIRST = 0.00088, 0.22, 1.56, 0.7, 4.8, 8.0 * 4.8 / 5.5
 KINDS0, KINDS, NBACT = "QVAQVA", "QAAQVA", True
 NQY, NQS, SGK = 2, 2, "va"
 VAL = {"0": 0, "1": 1, "2": 2, "4": 4, "9": 9, "a": 20, "b": 50, "c": 120}
-PRIO = ("920ac9219b009410122092c1440acb202c010009094c442290041420a2a24211929902bb440a90a00b1299a20244100b20bc100b00b04a99420ab0094ac01990124224402200200000000104940a900a099a04a42490000a02291290a420a410042221114b902102002499002b4204202000b224422902a220b04ab94040a1212014124100409004442202902909940204b19a0090c44a4902920b9949b0b40400b920a244200090000020000000400001001c042922900200910000010104010000100012010040000a000a0a00a90000000400010002042404410090209b424000400010020020000090014024b410b29b0204a2c42b902c4909102ac9424494090244c4baa04120222210094400baa20900190000042000290c004a0bb91")
+PRIO = ("440209b2c491a2214a2902200112190409a1a199ba4029c442209c2092a00cca9c9929424400a2a0194042109b2494410a9c2492bb9499021a009294994400040000904422094b29000bc9292c909440292b00049cb9241492c100b02441b0049c002c0b02122910004090949400291191014000190c90c420922291a44911c02200090400020494090920422049910090b2144109004901a00112b1b424949244420110411b22b004202040014020001a00192042012200112a0000010004222020412a94409400000901ac090ab2020900090000000204104012201000021902000114000001b004004044c44199049ccbb1a0224bca9c9b2a429000000240000142b10c990922221099a4012ac9a04b4092aa0b2009b1a9209090a2b0a2b")
 
 
 def cols(v, a, b, step=1):

@@ -8,11 +8,11 @@ ACT = {"id": ActivationFunctionType.Identity, "abs": ActivationFunctionType.Abs,
        "relu": ActivationFunctionType.Relu}
 SIZE = {"F": 4, "B": 2, "I": 4, "U": 2, "H": 2}
 DTYPE = {"F": "float32", "B": "bfloat16", "I": "int32", "U": "uint16", "H": "float16"}
-CYC, SEM, GAM, PEF, HOP2, HOP2FIRST = 0.00088, 0.22, 1.56, 0.7, 4.8, 8.0 * 4.8 / 5.5
-KINDS0, KINDS, NBACT = "QVAQVA", "QAAQVA", True
-NQY, NQS, SGK = 2, 2, "va"
+CYC, SEM, GAM, PEF, HOP2, HOP2FIRST = 0.0009, 0.25, 1.56, 0.7, 3.8, 8.0 * 3.8 / 5.5
+KINDS0, KINDS = "QVAQVA", "QAAQAA"
+NQY, NQS, SGK = 2, 2, "aa"
 VAL = {"0": 0, "1": 1, "2": 2, "4": 4, "9": 9, "a": 20, "b": 50, "c": 120}
-PRIO = ("440209b2c491a2214a2902200112190409a1a199ba4029c442209c2092a00cca9c9929424400a2a0194042109b2494410a9c2492bb9499021a009294994400040000904422094b29000bc9292c909440292b00049cb9241492c100b02441b0049c002c0b02122910004090949400291191014000190c90c420922291a44911c02200090400020494090920422049910090b2144109004901a00112b1b424949244420110411b22b004202040014020001a00192042012200112a0000010004222020412a94409400000901ac090ab2020900090000000204104012201000021902000114000001b004004044c44199049ccbb1a0224bca9c9b2a429000000240000142b10c990922221099a4012ac9a04b4092aa0b2009b1a9209090a2b0a2b")
+PRIO = ("14110b0c20a2402c01b44220a41c90a0a904200102b4022b00099c01022b021219bbc4921b9bb094202049b9c04cb92b109020c2c0940c09b9904021ba0a01100210c0bb404000a4249b4911144000bc9012021024110100042140a000044029241bb0c409b0a9020b04a220b929210499004900021002914000000000000000041c4400001000094002001000022441010a40200000100a242220029b000109010400024000000b04220440009429a4029aab900929014210b0020210000010040114040200099290400010b0000001924002049010010204200000920200401000010290221200000000001000a00c909121900b94290091029242a0a04b1b9004c42a410cb22cc4092249210b9a09022040ba402024441b194049ca24400200922a")
 
 
 def cols(v, a, b, step=1):
@@ -124,7 +124,8 @@ def build():
     s0I = rows(new("I", P), 0, 8); d0I = rows(new("I", P), 0, 32); drI = rows(new("I", 512), 0, 8)
     sgI = rows(new("I", 1024), 0, 32); lkI = new("I", 512)
     asko = [new("F", 64) for s in range(STEPS)]; aski = [new("F", 64) for s in range(STEPS)]
-    rpo = [new("H", 96) for s in range(STEPS)]; rpi = [new("H", 96) for s in range(STEPS)]
+    rw = [128] * (STEPS - 1) + [96]
+    rpo = [new("H", n) for n in rw]; rpi = [new("H", n) for n in rw]
 
     load("s", wtI, "wt", 2.2); load("a", s0I, "s0", 2.2); load("s", GB, "g0", 2.4); load("a", lkI, "lk", 3.0)
     load("s", d0I, "d0", 2.4); load("a", NM, "nm", 3.6); load("s", thI, "th", 2.4)
@@ -152,8 +153,9 @@ def build():
     Bh = new("H", 128); ts(Bh, c128(CG), rowg, "eq")
     B16 = new("B", 128); ts(B16, c128(CG), rowg, "eq", 0.0625, "mul")
     B16h = new("H", 128); ts(B16h, c128(CG), rowg, "eq", 0.0625, "mul")
+    N16h = new("H", 128); ts(N16h, c128(CG), rowg, "eq", -0.0625, "mul")
     Bf = new("F", 128); ts(Bf, c128(CG), rowg, "eq")
-    B224 = new("B", 128); ts(B224, c128(CG), rowg, "eq", float(W), "mul")
+    CPM = new("F", P); ts(CPM, cols(COL, 0, P), -float(W), "add")
     BP = new("B", 128); ts(BP, c128(CG), rowg, "eq", 1024.0, "mul")
     BN = new("B", 128); ts(BN, c128(CG), rowg, "eq", -1024.0, "mul")
     ONE = new("B", 256); mset(ONE, 1.0)
@@ -193,22 +195,13 @@ def build():
     SELS = [rows(new("H", 128), 0, 32) for c in range(4)]
     for c in range(4):
         ts(SELS[c], tH, float(-c), "eq")
-    WM = {}; WS = {}
-    for nm_, src, base, step in (("o", wtI, 7, -1), ("n", wnI, -8, 1)):
+    WM = {}
+    for nm_, src in (("o", wtI), ("n", wnI)):
         wf = new("F", 2); cp(wf, src)
         m4 = [new("B", 128) for k in range(4)]
         for k, (mat, c) in enumerate(((Bm, 0), (Bm, 1), (MA, 0), (MB, 0))):
             ts(m4[k], mat, cols(wf, c, c + 1), "mul")
         WM[nm_] = m4
-        part = new("B", 128); asel(part, Bm, [[0, 8], [step, 16]], "ge", 0.0, base, 0)
-        WS[nm_] = [new("B", 128) for j in range(2)]
-        for j in range(2):
-            ts(WS[nm_][j], part, cols(wf, j, j + 1), "mul")
-    SLOW = new("H", 128); SHIGH = new("H", 128); r0 = new("F", 1); r8 = new("F", 1)
-    ts(r0, rowa, 0.0, "eq"); ts(r8, rowa, 8.0, "eq"); ts(SLOW, Bm, r0, "mul"); ts(SHIGH, Bm, r8, "mul")
-    MROW2 = rows(new("B", 128), 0, 2); tY = rows(new("F", 128), 0, 2)
-    ts(tY, rows(MC, 0, 2), -1.0, "mul", 2048.0, "add")
-    ts(tY, tY, rows(rowf, 0, 2), "mul"); tt(MROW2, tY, rows(MC, 0, 2), "add")
     mset(cols(QB, P, W), 0.0); mset(cols(DK, P, W), 0.0); mset(cols(OK, P, W), -1.0); mset(cols(NF, P, W), 0.0)
     mset(cols(KB, P, W), 0.0); mset(cols(SLO, P, W), 0); mset(cols(SLN, P, W), 0)
     mset(cols(DRZ, 0, W), 0.0); mset(cols(LS, 0, W), 0.0); cp(cols(SG, 0, W), COL)
@@ -232,19 +225,28 @@ def build():
         for h in range(2):
             cp(cols(sgh, 512 * h, 512 * h + 512), cols(sgI, 512 * h, 512 * h + 512))
         for k in range(8):
-            pk = bank(2 + (k + 1) % 2, 0, 512)
+            pk = bank((k + 3) % 4, 0, 512)
             mm([(pk, SELS[k // 2], cols(sgh, 512 * (k % 2), 512 * (k % 2) + 512))])
             act(cols(SGT, 512 * k, 512 * k + 512), pk, "id", float(W))
 
     def scratch(n, nh):
         return {"r": new("I", n), "x": new("H", n), "sc": new("F", n), "co": new("U", max(2, n // 16)),
-                "xs": new("F", n), "u": new("I", 2 * nh), "u2": new("I", 2 * nh), "h": new("I", nh), "h2": new("I", nh)}
+                "xs": new("F", n), "u": new("I", 2 * nh), "u2": new("I", 2 * nh), "h": new("I", nh), "h2": new("I", nh),
+                "l": new("I", nh), "l2": new("I", nh), "l3": new("F", nh)}
 
-    def wish(S, n, G, K, q, p1, p2, half):
+    def row_rho(out, r, y, n, G, mat):
+        mm([(y, NI, rows(cols(ONE, 0, n), 0, 1))], stop=False); mm([(y, mat, G)], start=False)
+        cp(r, y); tt(out, r, y, "eq")
+
+    def wish(S, n, G, K, q, p1, p2, oh):
         y = bank(p1, 0, n); c = bank(p2, 0, n)
-        mm([(y, NI, rows(cols(ONE, 0, n), 0, 1))], stop=False); mm([(y, B16h if half else B16, G)], start=False)
-        cp(S["r"], y); tt(y, S["r"], y, "eq"); tt(S["x"], K, y, "mul")
-        mm([(c, ML, cols(MR, 0, n))], stop=False); mm([(c, Bh, S["x"])], start=False)
+        if oh:
+            tt(S["x"], K, oh, "mul")
+            mm([(c, ML, cols(MR, 0, n)), (c, N16h, f1)], stop=False)
+        else:
+            row_rho(y, S["r"], y, n, G, B16); tt(S["x"], K, y, "mul")
+            mm([(c, ML, cols(MR, 0, n))], stop=False)
+        mm([(c, Bh, S["x"])], start=False)
         scan(S["sc"], cols(RS0, 0, n), c, 0.0, "mul", "max"); cp(S["co"], cols(S["sc"], 15, n, 16))
         tt(S["xs"], ind(NM, S["co"]), G, "add")
         ts(y, S["xs"], 256.0, "ge", -256.0, "mul"); tt(q, S["xs"], y, "add")
@@ -260,42 +262,27 @@ def build():
             mm([(o, WM[w][2], q), (o, WM[w][3], q)], start=False)
         u, u2, h, h2 = cols(S["u"], 0, 2 * m), cols(S["u2"], 0, 2 * m), cols(S["h"], 0, m), cols(S["h2"], 0, m)
         cp(u, bank(pu, 0, 2 * m)); ts(u2, u, 4095, "and")
-        tt(h, cols(u2, 0, m), cols(u2, m, 2 * m), "mul"); ts(h2, h, 5, "shr")
-        tt(h, h2, bank(pl, 0, m), "add"); ts(out, h, 4095, "and")
+        tt(h, cols(u2, 0, m), cols(u2, m, 2 * m), "mul")
+        l, l2, l3 = (cols(S[x], 0, m) for x in ("l", "l2", "l3"))
+        cp(l, bank(pl, 0, m)); ts(l2, l, 4095, "and"); ts(l3, l2, 32.0, "mul", -131072.0, "add")
+        tt(h2, h, l3, "add"); ts(out, h2, 5, "shr", 4095, "and")
 
     H = P // 2
     SB = [scratch(H, H) for h in range(2)]; SN = [scratch(16, H) for h in range(2)]; SY = scratch(32, 64)
     offB = new("U", P); QR = new("B", 16 * P); DF = new("B", 16 * P)
-    QT = rows(new("B", 256), 0, 96); hh = new("H", P)
+    QT = rows(new("B", 256), 0, 96)
 
-    def slots_both(h, q, D, bx, by):
-        one = rows(cols(ONE, 0, H), 0, 2); S = SB[h]; hq = cols(hh, H * h, H * h + H)
-        lin = lambda o, w: [(o, MROW2, one), (o, I608, D), (o, I5, D), (o, w[2], q), (o, w[3], q)]
-        mm([(bank(bx, j * H, j * H + H), WS[w][j], q) for j in range(2) for w in "on"])
-        o = bank(by, 0, H); o2 = bank(bx, 0, H)
-        mm(lin(o, WM["o"]), stop=False)
-        cp(S["u"], bank(bx, 0, 2 * H)); ts(S["u2"], S["u"], 4095, "and")
-        mm(lin(o2, WM["n"]), stop=False)
-        tt(S["h"], cols(S["u2"], 0, H), cols(S["u2"], H, 2 * H), "mul")
-        ts(S["h2"], S["h"], 5, "shr", 4095, "and"); ts(hq, S["h2"], -2048.0, "add")
-        mm([(o, SLOW, hq)], start=False); mm([(o2, SHIGH, hq)], start=False)
-        cp(S["h"], o); ts(cols(SLO, H * h, H * h + H), S["h"], 4095, "and")
-        cp(SN[h]["h"], o2); ts(cols(SLN, H * h, H * h + H), SN[h]["h"], 4095, "and")
-
-    def big_look(h, kinds, both):
+    def big_look(h, kinds):
         a0, a1 = H * h, H * h + H
         half = lambda v: cols(v, a0, a1)
         bx, by = 4 + 2 * h, 5 + 2 * h
         q = half(QB); D = half(DK)
-        wish(SB[h], H, half(GB), half(KN), q, bx, by, False)
+        wish(SB[h], H, half(GB), half(KN), q, bx, by, None)
         act(half(KB), half(KN), "id")
         if kinds[3 * h:3 * h + 3] != "QQQ":
             mm([(rows(bank(by, 0, 128), 0, 96), q, NID)])
             act(cols(QT, 128 * h, 128 * h + 128), rows(bank(by, 0, 128), 0, 96), "id")
-        if both:
-            slots_both(h, q, D, bx, by)
-        else:
-            slots(SB[h], H, q, D, "o", half(SLO), bx, by)
+        slots(SB[h], H, q, D, "o", half(SLO), bx, by)
         cp(half(offB), half(SLO))
         for c in range(3 * h, 3 * h + 3):
             if kinds[c] == "Q":
@@ -305,43 +292,43 @@ def build():
                     tt(cols(DF, x, y), ind(TAB, cols(offB, a, a + 16)), cols(QR, x, y), "sub")
                     act(cols(DF, x, y), cols(DF, x, y), "abs")
             else:
-                o = bank(by, 0, 512); j = 32 * (c % 3); eg = cols(QR, 512 * c, 512 * c + 512)
+                o = bank(bx if kinds[3 * h:c].strip("Q") else by, 0, 512)
+                j = 32 * (c % 3); eg = cols(QR, 512 * c, 512 * c + 512)
                 for a in (0, 16):
                     src = ind(TAB, cols(offB, 32 * c + a, 32 * c + a + 16)); dst = cols(eg, 16 * a, 16 * a + 256)
                     act(dst, src, "id") if kinds[c] == "A" else cp(dst, src)
                 mm([(o, rows(cols(QT, 128 * h, 128 * h + 128), j, j + 32), rows(RR, j, j + 32))], stop=False)
                 mm([(o, Id, eg)], start=False)
                 act(cols(DF, 512 * c, 512 * c + 512), o, "abs")
-        if not both:
-            slots(SN[h], H, q, D, "n", half(SLN), bx, by)
+        slots(SN[h], H, q, D, "n", half(SLN), bx, by)
         o = bank(bx, 0, H)
         mm([(o, cols(UM, 15 - r, 143 - r), cols(DF, 16 * a0 + r, 16 * a1, 16)) for r in range(16)])
         act(half(OK), o, "sign", thp, -1.0)
         mm([(o, Bm, half(OK))]); act(half(NF), o, "sign", -16.0, -1.0)
 
-    first = new("B", P); fs = new("F", P); sm = new("F", P); dtm = new("B", P); dts = new("B", P)
-    mx = [new("F", 6) for h in range(2)]; offG = [new("U", 6) for h in range(2)]; offS = [new("U", 6) for h in range(2)]
+    slp = new("F", P); fs = new("F", P); sm = new("F", P); dtm = new("B", P); dts = new("F", P)
+    offG = [new("U", 6) for h in range(2)]; offS = [new("U", 6) for h in range(2)]
 
     def big_update(h):
         half = lambda v: cols(v, H * h, H * h + H)
         x, o = bank(4 + 2 * h, 0, H), bank(5 + 2 * h, 0, H)
         sc = half(sc_b); last = cols(sc, 15, H, 16)
-        mm([(x, TRI, half(OK))]); act(half(first), x, "relu", tbias, -0.5)
-        act(x, x, "relu", tbias, -0.5)
-        tt(half(fs), half(SLO), x, "mul")
-        mm([(o, ML, cols(MR, 0, H)), (o, B224, half(first))], stop=False); mm([(o, Bf, half(fs))], start=False)
-        scan(sc, cols(RS0, 0, H), o, 0.0, "mul", "max")
-        tt(mx[h], last, cols(PW, 6 * h, 6 * h + 6), "max"); cp(offG[h], mx[h])
+        mm([(o, DM, half(DK))]); tt(half(dtm), o, half(NF), "mul")
+        tt(half(slp), half(SLO), half(CPM), "sub")
+        mm([(x, TRI, half(OK))]); act(x, x, "relu", tbias, -0.5)
+        tt(half(fs), half(slp), x, "mul")
+        mm([(o, ML, cols(MR, 0, H)), (o, rows(c128(ONE), 0, 1), rows(half(COL), 0, 1))], stop=False)
+        mm([(o, Bf, half(fs))], start=False)
+        scan(sc, cols(RS0, 0, H), o, 0.0, "mul", "max"); cp(offG[h], last)
         tt(half(sm), ind(SG, offG[h]), cols(MK, 0, H), "mul")
         act(half(GB), ind(ENT, offG[h]), "id")
         scan(sc, cols(RS0, 0, H), half(sm), 0.0, "mul", "max"); cp(offS[h], last)
         act(half(KN), ind(KW, offS[h]), "id")
-        mm([(x, DM, half(DK))]); tt(half(dtm), x, half(NF), "mul")
-        act(half(dts), ind(DRZ, offS[h]), "id")
-        mm([(x, Id, half(DK)), (x, NID, half(dtm))], stop=False); mm([(x, Id, half(dts))], start=False); act(half(DK), x, "id")
+        tt(half(dts), ind(DRZ, offS[h]), half(DK), "add"); tt(half(DK), half(dts), half(dtm), "sub")
 
     kold = new("F", 32); dold = new("B", 32); dlt = new("B", 32); vy = new("F", 32)
-    f1 = new("F", 32); kt = new("F", 32); ky = new("F", 32); dy1 = new("F", 32); dyt = new("F", 32); dy = new("B", 32)
+    f1 = new("H", 32); r2 = new("I", 32)
+    kt = new("F", 32); ky = new("F", 32); dy1 = new("F", 32); dyt = new("F", 32); dy = new("B", 32)
     qy = new("B", 32); sly = new("I", 64); offY = new("U", 32); oky = new("B", 32)
     QS = new("B", 512); AS = new("B", 512); st = new("F", 512); DY = new("B", 512)
     cnt = new("F", W); junk = [new("B", W) for b in range(2)]; acc = new("F", 2)
@@ -357,7 +344,7 @@ def build():
         L = lst[s - 1]
         G = merge(s - 1)
         tt(ky, kt, f1, "sub"); tt(dy, dy1, dyt, "add")
-        wish(SY, 32, G, ky, qy, 2, 3, True)
+        wish(SY, 32, G, kt, qy, 2, 3, cols(rpi[s - 1], 96, 128))
         slots(SY, 32, qy, dy, "on", sly, 2, 3)
         cp(offY, cols(sly, 0, 32))
         n = 32 // NQY
@@ -408,19 +395,21 @@ def build():
         cp(idx, cols(st, 255, 512, 256))
         tt(sm2, ind(SW, idx), cols(MK, 0, 32), "mul")
         tt(cols(rpo[s], 0, 32), ind(DW, idx), q, "add")
+        if s < STEPS - 1:
+            row_rho(cols(rpo[s], 96, 128), r2, bank(2, 0, 32), 32, cols(rpo[s], 0, 32), B16h)
         scan(sc2, cols(RS0, 0, 32), sm2, 0.0, "mul", "max"); cp(of2, cols(sc2, 15, 32, 16))
         cp(cols(rpo[s], 32, 64), ind(LS, of2)); cp(cols(rpo[s], 64, 96), ind(DRZ, of2))
         send("mr%d" % s, rpo[s], rpi[s], False, HOP2)
 
     for s in range(STEPS):
+        if s == 0:
+            tables()
         marks.append(len(ops))
         for h in range(2):
-            big_look(h, KINDS if s else KINDS0, NBACT and s > 0)
+            big_look(h, KINDS if s else KINDS0)
         if s:
             small_look(s)
         ask(s)
-        if s == 0:
-            tables()
         serve(s)
         big_update(0); big_update(1)
     marks.append(len(ops))
@@ -428,7 +417,7 @@ def build():
     mset(cols(OG, P, W), 0.0); mset(cols(OD, P, W), 0.0)
     act(cols(KB, 0, P), KN, "id"); act(cols(OG, 0, P), GB, "id"); act(cols(OD, 0, P), cols(DK, 0, P), "id")
     G = merge(STEPS - 1)
-    cp(ind(OG, L), G); tt(ind(KB, L), kt, f1, "sub"); tt(ind(OD, L), dy1, dyt, "add")
+    cp(ind(OG, L), G); tt(ky, kt, f1, "sub"); cp(ind(KB, L), ky); tt(ind(OD, L), dy1, dyt, "add")
 
     def store(q, name, a, src):
         add(q, "store", (name, a, src), [src], [], 0.1, 2.2)
@@ -493,6 +482,14 @@ def schedule(ops, wts=None):
     return sorted(range(n), key=lambda i: (ops[i]["t"], i))
 
 
+def needed(ops, order):
+    live = set(i for i, o in enumerate(ops) if o["kind"] in ("store", "send", "recv"))
+    for i in range(len(ops) - 1, -1, -1):
+        if i in live:
+            live |= ops[i]["deps"]
+    return [i for i in order if i in live]
+
+
 def syncs(ops, order):
     pos = {}
     known = {}
@@ -539,7 +536,7 @@ def syncs(ops, order):
 
 OPS, TOP = build()
 depend(OPS)
-ORDER = schedule(OPS, [VAL[c] for c in PRIO])
+ORDER = needed(OPS, schedule(OPS, [VAL[c] for c in PRIO]))
 FINAL = syncs(OPS, ORDER)
 MSGS = [OPS[i]["args"] for i in ORDER if OPS[i]["kind"] == "send"]
 

from concourse.mybir import AluOpType, ActivationFunctionType

P, W, NS, STEPS = 192, 224, 4096, 6
ALU = {"add": AluOpType.add, "sub": AluOpType.subtract, "mul": AluOpType.mult, "max": AluOpType.max, "min": AluOpType.min,
       "ge": AluOpType.is_ge, "lt": AluOpType.is_lt, "eq": AluOpType.is_equal, "ne": AluOpType.not_equal,
       "shr": AluOpType.arith_shift_right, "and": AluOpType.bitwise_and}
ACT = {"id": ActivationFunctionType.Identity, "abs": ActivationFunctionType.Abs, "sign": ActivationFunctionType.Sign,
       "relu": ActivationFunctionType.Relu}
SIZE = {"F": 4, "B": 2, "I": 4, "U": 2, "H": 2}
DTYPE = {"F": "float32", "B": "bfloat16", "I": "int32", "U": "uint16", "H": "float16"}
CYC, SEM, GAM, PEF, HOP2, HOP2FIRST = 0.0009, 0.25, 1.56, 0.7, 3.8, 8.0 * 3.8 / 5.5
KINDS0, KINDS = "QVAQVA", "QAAQAA"
NQY, NQS, SGK = 2, 2, "aa"
VAL = {"0": 0, "1": 1, "2": 2, "4": 4, "9": 9, "a": 20, "b": 50, "c": 120}
PRIO = ("14110b0c20a2402c01b44220a41c90a0a904200102b4022b00099c01022b021219bbc4921b9bb094202049b9c04cb92b109020c2c0940c09b9904021ba0a01100210c0bb404000a4249b4911144000bc9012021024110100042140a000044029241bb0c409b0a9020b04a220b929210499004900021002914000000000000000041c4400001000094002001000022441010a40200000100a242220029b000109010400024000000b04220440009429a4029aab900929014210b0020210000010040114040200099290400010b0000001924002049010010204200000920200401000010290221200000000001000a00c909121900b94290091029242a0a04b1b9004c42a410cb22cc4092249210b9a09022040ba402024441b194049ca24400200922a")


def cols(v, a, b, step=1):
    return (v[0], v[1] + a, v[1] + b, step, v[4], v[5], v[6])


def rows(v, a, b, step=1):
    return (v[0], v[1], v[2], v[3], a, b, step)


def width(v):
    return (v[2] - v[1] + v[3] - 1) // v[3]


def ind(win, off):
    return ("ind", win, off)


def build():
    top = {k: 0 for k in SIZE}
    ops = []
    marks = []

    def new(kind, n):
        al = 32 // SIZE[kind]
        a = top[kind]
        top[kind] = (a + n + al - 1) // al * al
        return (kind, a, a + n, 1, 0, 128, 1)

    def bank(i, a, b):
        return ("P%d" % i, a, b, 1, 0, 128, 1)

    def parts(x):
        if isinstance(x, tuple):
            return [x[1], x[2]] if x[0] == "ind" else [x]
        return []

    def add(eng, kind, args, rd, wr, dur, lat=None):
        r = [v for x in rd for v in parts(x)]
        w = []
        for x in wr:
            if x[0] == "ind":
                w.append(x[1]); r.append(x[2])
            else:
                w.append(x)
        ops.append({"eng": eng, "kind": kind, "args": args, "r": r, "w": w, "dur": dur, "lat": dur if lat is None else lat})
        return len(ops) - 1

    def cost(out, ins, two=False):
        if out[0] == "ind":
            return 0.05 + 16 * width(out[2]) * 3.8 * CYC
        if ins[0][0] == "ind":
            return 0.06 + width(out) * GAM * CYC
        n = width(ins[0])
        if two:
            n *= 2 if all(x[0][0] != "P" for x in ins) else 1
        elif SIZE.get(out[0], 4) == 2 and SIZE.get(ins[0][0], 4) == 2:
            n /= 2
        return max(64, n) * CYC

    def cp(out, a):
        return add("v", "cp", (out, a), [a], [out], cost(out, [a]))

    def tt(out, a, b, op):
        return add("v", "tt", (out, a, b, op), [a, b], [out], cost(out, [a, b], True))

    def ts(out, a, s1, op0, s2=None, op1=None):
        return add("v", "ts", (out, a, s1, s2, op0, op1), [a, s1, s2], [out], cost(out, [a]))

    def scan(out, a, b, init, op0, op1):
        return add("v", "scan", (out, a, b, init, op0, op1), [a, b, init], [out], max(64, width(out)) * CYC)

    def mset(out, c):
        return add("v", "mset", (out, c), [], [out], max(64, width(out) * SIZE[out[0]] / 4) * CYC)

    def act(out, a, f, bias=0.0, scale=1.0, acc=None):
        d = 0.07 + width(out) * GAM * CYC if a[0] == "ind" else max(64, width(out)) * CYC
        return add("a", "act", (out, a, f, bias, scale, acc), [a, bias, scale], [out] + ([acc] if acc else []), d)

    def mm(lst, start=True, stop=True):
        seq = []
        for i, (o, l, r) in enumerate(lst):
            first = start and all(x[0] != o for x in lst[:i])
            last = stop and all(x[0] != o for x in lst[i + 1:])
            seq.append((o, l, r, first, last))
        d = sum(max(64, width(r)) * (4 if r[0] == "F" else 1) for o, l, r in lst) * CYC * PEF
        return add("t", "mm", seq, [x for o, l, r in lst for x in (l, r)], [o for o, l, r in lst], d)

    def iota(out, pat, base, cm):
        return add("g", "iota", (out, pat, base, cm), [], [out], 0.13 + 2 * width(out) * CYC)

    def asel(out, a, pat, op, fill, base, cm):
        return add("g", "asel", (out, a, pat, op, fill, base, cm), [a], [out], 0.17 + 2 * width(out) * CYC)

    def load(q, out, name, lat):
        return add(q, "load", (out, name), [], [out], 0.1, lat)

    def send(name, src, dst, nxt, lat):
        i = add("g", "send", (name, src, dst, nxt), [src], [], 0.4)
        j = add(None, "recv", (name,), [], [dst], 0.0, 0.0)
        ops[j]["after"] = (i, lat)

    ENT = new("B", W + NS); QB = cols(ENT, 0, W); TAB = cols(ENT, W, W + NS)
    NM = new("B", 1024); GB = new("B", P); DK = new("B", W); DRZ = new("B", W + 512); OK = new("B", W)
    SG = new("F", W + NS); SGT = cols(SG, W, W + NS)
    KW = new("F", W + 512); KB = cols(KW, 0, W); LS = new("F", W + 512); NF = new("F", W); KN = new("F", P)
    SL = new("I", 2 * W); SLO = cols(SL, 0, W); SLN = cols(SL, W, 2 * W)
    wtI = new("I", 2); wnI = new("I", 2); thI = new("I", 1)
    s0I = rows(new("I", P), 0, 8); d0I = rows(new("I", P), 0, 32); drI = rows(new("I", 512), 0, 8)
    sgI = rows(new("I", 1024), 0, 32); lkI = new("I", 512)
    asko = [new("F", 64) for s in range(STEPS)]; aski = [new("F", 64) for s in range(STEPS)]
    rw = [128] * (STEPS - 1) + [96]
    rpo = [new("H", n) for n in rw]; rpi = [new("H", n) for n in rw]

    load("s", wtI, "wt", 2.2); load("a", s0I, "s0", 2.2); load("s", GB, "g0", 2.4); load("a", lkI, "lk", 3.0)
    load("s", d0I, "d0", 2.4); load("a", NM, "nm", 3.6); load("s", thI, "th", 2.4)
    load("a", sgI, "sg", 4.0); load("a", drI, "dr", 4.0); load("s", TAB, "ent", 8.0)
    send("mw", wtI, wnI, False, HOP2FIRST)

    rowI = new("I", 1); iota(rowI, [[0, 1]], 0, 1)
    CA = new("B", 256); iota(CA, [[0, 16], [1, 16]], 0, 0)
    CG = new("B", 256); iota(CG, [[1, 16], [0, 16]], 0, 0)
    COL = new("B", W); iota(COL, [[1, W]], 0, 0)
    MC = new("B", 128); iota(MC, [[0, 32], [-1, 4]], 3, 0)
    S32 = new("B", 128); iota(S32, [[4, 8], [-1, 4], [0, 4]], 3, 0)
    POS = new("F", 512); iota(POS, [[1, 512]], 32, 0)
    tI = new("I", 2); rowf = new("F", 1); rowa = new("F", 1); rowg = new("F", 1)
    cp(rowf, rowI)
    ts(cols(tI, 0, 1), rowI, 15, "and"); cp(rowa, cols(tI, 0, 1))
    ts(cols(tI, 1, 2), rowI, 4, "shr"); cp(rowg, cols(tI, 1, 2))
    c128 = lambda v: cols(v, 0, 128)
    MK = new("B", 256); ts(MK, CA, rowa, "eq")
    ML = rows(c128(MK), 0, 16)
    MR = rows(new("B", P), 0, 16); ts(MR, rows(cols(MK, 0, P), 0, 16), -1.0, "add", 32768.0, "mul")
    RS0 = new("B", 256); ts(RS0, CA, 0.0, "ne")
    SEL8 = rows(new("H", 128), 0, 8); ts(SEL8, rows(c128(CG), 0, 8), rows(rowf, 0, 8), "eq")
    Bm = new("B", 128); ts(Bm, c128(CG), rowg, "eq")
    Bh = new("H", 128); ts(Bh, c128(CG), rowg, "eq")
    B16 = new("B", 128); ts(B16, c128(CG), rowg, "eq", 0.0625, "mul")
    B16h = new("H", 128); ts(B16h, c128(CG), rowg, "eq", 0.0625, "mul")
    N16h = new("H", 128); ts(N16h, c128(CG), rowg, "eq", -0.0625, "mul")
    Bf = new("F", 128); ts(Bf, c128(CG), rowg, "eq")
    CPM = new("F", P); ts(CPM, cols(COL, 0, P), -float(W), "add")
    BP = new("B", 128); ts(BP, c128(CG), rowg, "eq", 1024.0, "mul")
    BN = new("B", 128); ts(BN, c128(CG), rowg, "eq", -1024.0, "mul")
    ONE = new("B", 256); mset(ONE, 1.0)
    ONEF = new("F", W); mset(ONEF, 1.0)
    NI = rows(new("B", 128), 0, 1); ts(NI, rows(c128(CA), 0, 1), -0.0625, "mul")
    MROW = rows(new("B", 128), 0, 1); cp(MROW, rows(MC, 0, 1))
    I608 = new("B", 128); ts(I608, c128(COL), rowf, "eq", 608.0, "mul")
    I5 = new("B", 128); ts(I5, c128(COL), rowf, "eq", 5.0, "mul")
    SEL32 = rows(new("H", 128), 0, 32); ts(SEL32, rows(S32, 0, 32), rows(rowf, 0, 32), "eq")
    tA = new("B", 128); tB = new("B", 128); MA = new("B", 128); MB = new("B", 128)
    ts(tA, MC, 2.0, "mul", 4.0, "min"); tt(MA, tA, Bm, "mul")
    ts(tB, MC, 3.0, "eq", 2.0, "mul"); tt(MB, tB, Bm, "mul")
    REPO = new("U", P); ts(REPO, cols(POS, 0, P), -32.0, "add")
    ucol = new("F", 1); ts(ucol, rowg, 16.0, "mul", 15.0, "add")
    UM = new("B", 144); ts(UM, cols(COL, 0, 144), ucol, "eq")
    thF = new("F", 1); thp = new("F", 1); pt0 = new("F", 1); pt1 = new("F", 1); PT = new("B", 256)
    cp(thF, thI); ts(thp, thF, 0.5, "add")
    ts(pt0, rowa, -256.0, "mul", thF, "add"); ts(pt1, pt0, 1.0, "add", 0.0, "max")
    ts(PT, ONE, pt1, "mul", 256.0, "min")
    MR2 = rows(new("B", 256), 0, 16); ts(MR2, rows(CG, 0, 16), rows(rowf, 0, 16), "ne", -8388608.0, "mul")
    PW = new("F", 12); ts(PW, cols(COL, 0, 12), 16.0, "mul", rowa, "add")
    JB = new("F", 2); ts(JB, cols(PW, 0, 2), 0.5, "add")
    Id = new("B", 128); ts(Id, c128(COL), rowf, "eq")
    NID = new("B", 128); ts(NID, c128(COL), rowf, "eq", -1.0, "mul")
    tI3 = new("I", 1); row32 = new("F", 1); RR = new("B", 512)
    ts(tI3, rowI, 31, "and"); cp(row32, tI3)
    ts(cols(RR, 0, 256), CG, row32, "eq"); ts(cols(RR, 256, 512), CG, row32, "sub", -16.0, "eq")
    tC = new("B", 128); TRI = new("B", 128)
    asel(tC, Bm, [[-1, 128]], "ge", 0.0, 0, 1); asel(TRI, tC, [[-1, 128]], "ne", -1.0, 0, 1)
    tbias = new("F", 1); ts(tbias, rowa, 0.5, "mul", -7.0, "add")
    tF = new("B", 128); DM = new("B", 128)
    asel(tF, Bm, [[-1, 128]], "eq", 0.0, -4, 1); asel(DM, tF, [[-1, 128]], "ne", -1.0, 0, 1)
    VC = new("F", W); ts(VC, COL, float(P), "lt", -1.0, "mul")
    tG = rows(new("B", 128), 0, 8); SELD = rows(new("H", 128), 0, 8)
    ts(tG, rows(c128(CA), 0, 8), 12.0, "ge"); tt(SELD, tG, SEL8, "mul")
    tH = rows(new("B", 128), 0, 32); ts(tH, rows(c128(CG), 0, 32), 4.0, "mul", rows(rowf, 0, 32), "sub")
    SELS = [rows(new("H", 128), 0, 32) for c in range(4)]
    for c in range(4):
        ts(SELS[c], tH, float(-c), "eq")
    WM = {}
    for nm_, src in (("o", wtI), ("n", wnI)):
        wf = new("F", 2); cp(wf, src)
        m4 = [new("B", 128) for k in range(4)]
        for k, (mat, c) in enumerate(((Bm, 0), (Bm, 1), (MA, 0), (MB, 0))):
            ts(m4[k], mat, cols(wf, c, c + 1), "mul")
        WM[nm_] = m4
    mset(cols(QB, P, W), 0.0); mset(cols(DK, P, W), 0.0); mset(cols(OK, P, W), -1.0); mset(cols(NF, P, W), 0.0)
    mset(cols(KB, P, W), 0.0); mset(cols(SLO, P, W), 0); mset(cols(SLN, P, W), 0)
    mset(cols(DRZ, 0, W), 0.0); mset(cols(LS, 0, W), 0.0); cp(cols(SG, 0, W), COL)
    DW = new("B", 544); SW = new("F", 544); mset(cols(DW, 0, 32), 0.0); mset(cols(SW, 0, 32), 0.0)

    cp(cols(KW, W, W + 512), lkI)
    sc_b = new("F", P); s0h = rows(new("H", P), 0, 8); off0 = new("U", 12)
    cp(s0h, s0I)
    pb = bank(4, 0, P)
    mm([(pb, ML, MR)], stop=False); mm([(pb, SEL8, s0h)], start=False)
    scan(sc_b, cols(RS0, 0, P), pb, 0.0, "mul", "max"); cp(off0, cols(sc_b, 15, P, 16))
    cp(KN, ind(cols(KW, W, W + 512), off0))
    d0h = rows(new("H", P), 0, 32); cp(d0h, d0I)
    mm([(bank(5, 0, P), SEL32, d0h)]); act(cols(DK, 0, P), bank(5, 0, P), "id")

    def tables():
        act(cols(LS, W, W + 512), cols(KW, W, W + 512), "id", 1024.0)
        drh = rows(new("H", 512), 0, 8); cp(drh, drI)
        mm([(bank(2, 0, 512), SELD, drh)]); act(cols(DRZ, W, W + 512), bank(2, 0, 512), "id")
        sgh = rows(new("H", 1024), 0, 32)
        for h in range(2):
            cp(cols(sgh, 512 * h, 512 * h + 512), cols(sgI, 512 * h, 512 * h + 512))
        for k in range(8):
            pk = bank((k + 3) % 4, 0, 512)
            mm([(pk, SELS[k // 2], cols(sgh, 512 * (k % 2), 512 * (k % 2) + 512))])
            act(cols(SGT, 512 * k, 512 * k + 512), pk, "id", float(W))

    def scratch(n, nh):
        return {"r": new("I", n), "x": new("H", n), "sc": new("F", n), "co": new("U", max(2, n // 16)),
                "xs": new("F", n), "u": new("I", 2 * nh), "u2": new("I", 2 * nh), "h": new("I", nh), "h2": new("I", nh),
                "l": new("I", nh), "l2": new("I", nh), "l3": new("F", nh)}

    def row_rho(out, r, y, n, G, mat):
        mm([(y, NI, rows(cols(ONE, 0, n), 0, 1))], stop=False); mm([(y, mat, G)], start=False)
        cp(r, y); tt(out, r, y, "eq")

    def wish(S, n, G, K, q, p1, p2, oh):
        y = bank(p1, 0, n); c = bank(p2, 0, n)
        if oh:
            tt(S["x"], K, oh, "mul")
            mm([(c, ML, cols(MR, 0, n)), (c, N16h, f1)], stop=False)
        else:
            row_rho(y, S["r"], y, n, G, B16); tt(S["x"], K, y, "mul")
            mm([(c, ML, cols(MR, 0, n))], stop=False)
        mm([(c, Bh, S["x"])], start=False)
        scan(S["sc"], cols(RS0, 0, n), c, 0.0, "mul", "max"); cp(S["co"], cols(S["sc"], 15, n, 16))
        tt(S["xs"], ind(NM, S["co"]), G, "add")
        ts(y, S["xs"], 256.0, "ge", -256.0, "mul"); tt(q, S["xs"], y, "add")

    def slots(S, n, q, D, who, out, pu, pl):
        m = n * len(who)
        for k, w in enumerate(who):
            o = bank(pl, k * n, k * n + n)
            mm([(o, MROW, rows(cols(ONE, 0, n), 0, 1)), (o, I608, D), (o, I5, D)], stop=False)
            if k == 0:
                mm([(bank(pu, (j * len(who) + kk) * n, (j * len(who) + kk + 1) * n), WM[ww][j], q)
                    for j in range(2) for kk, ww in enumerate(who)])
            mm([(o, WM[w][2], q), (o, WM[w][3], q)], start=False)
        u, u2, h, h2 = cols(S["u"], 0, 2 * m), cols(S["u2"], 0, 2 * m), cols(S["h"], 0, m), cols(S["h2"], 0, m)
        cp(u, bank(pu, 0, 2 * m)); ts(u2, u, 4095, "and")
        tt(h, cols(u2, 0, m), cols(u2, m, 2 * m), "mul")
        l, l2, l3 = (cols(S[x], 0, m) for x in ("l", "l2", "l3"))
        cp(l, bank(pl, 0, m)); ts(l2, l, 4095, "and"); ts(l3, l2, 32.0, "mul", -131072.0, "add")
        tt(h2, h, l3, "add"); ts(out, h2, 5, "shr", 4095, "and")

    H = P // 2
    SB = [scratch(H, H) for h in range(2)]; SN = [scratch(16, H) for h in range(2)]; SY = scratch(32, 64)
    offB = new("U", P); QR = new("B", 16 * P); DF = new("B", 16 * P)
    QT = rows(new("B", 256), 0, 96)

    def big_look(h, kinds):
        a0, a1 = H * h, H * h + H
        half = lambda v: cols(v, a0, a1)
        bx, by = 4 + 2 * h, 5 + 2 * h
        q = half(QB); D = half(DK)
        wish(SB[h], H, half(GB), half(KN), q, bx, by, None)
        act(half(KB), half(KN), "id")
        if kinds[3 * h:3 * h + 3] != "QQQ":
            mm([(rows(bank(by, 0, 128), 0, 96), q, NID)])
            act(cols(QT, 128 * h, 128 * h + 128), rows(bank(by, 0, 128), 0, 96), "id")
        slots(SB[h], H, q, D, "o", half(SLO), bx, by)
        cp(half(offB), half(SLO))
        for c in range(3 * h, 3 * h + 3):
            if kinds[c] == "Q":
                for a in (32 * c, 32 * c + 16):
                    x, y = 16 * a, 16 * a + 256
                    act(cols(QR, x, y), ind(q, cols(REPO, a - a0, a - a0 + 16)), "id")
                    tt(cols(DF, x, y), ind(TAB, cols(offB, a, a + 16)), cols(QR, x, y), "sub")
                    act(cols(DF, x, y), cols(DF, x, y), "abs")
            else:
                o = bank(bx if kinds[3 * h:c].strip("Q") else by, 0, 512)
                j = 32 * (c % 3); eg = cols(QR, 512 * c, 512 * c + 512)
                for a in (0, 16):
                    src = ind(TAB, cols(offB, 32 * c + a, 32 * c + a + 16)); dst = cols(eg, 16 * a, 16 * a + 256)
                    act(dst, src, "id") if kinds[c] == "A" else cp(dst, src)
                mm([(o, rows(cols(QT, 128 * h, 128 * h + 128), j, j + 32), rows(RR, j, j + 32))], stop=False)
                mm([(o, Id, eg)], start=False)
                act(cols(DF, 512 * c, 512 * c + 512), o, "abs")
        slots(SN[h], H, q, D, "n", half(SLN), bx, by)
        o = bank(bx, 0, H)
        mm([(o, cols(UM, 15 - r, 143 - r), cols(DF, 16 * a0 + r, 16 * a1, 16)) for r in range(16)])
        act(half(OK), o, "sign", thp, -1.0)
        mm([(o, Bm, half(OK))]); act(half(NF), o, "sign", -16.0, -1.0)

    slp = new("F", P); fs = new("F", P); sm = new("F", P); dtm = new("B", P); dts = new("F", P)
    offG = [new("U", 6) for h in range(2)]; offS = [new("U", 6) for h in range(2)]

    def big_update(h):
        half = lambda v: cols(v, H * h, H * h + H)
        x, o = bank(4 + 2 * h, 0, H), bank(5 + 2 * h, 0, H)
        sc = half(sc_b); last = cols(sc, 15, H, 16)
        mm([(o, DM, half(DK))]); tt(half(dtm), o, half(NF), "mul")
        tt(half(slp), half(SLO), half(CPM), "sub")
        mm([(x, TRI, half(OK))]); act(x, x, "relu", tbias, -0.5)
        tt(half(fs), half(slp), x, "mul")
        mm([(o, ML, cols(MR, 0, H)), (o, rows(c128(ONE), 0, 1), rows(half(COL), 0, 1))], stop=False)
        mm([(o, Bf, half(fs))], start=False)
        scan(sc, cols(RS0, 0, H), o, 0.0, "mul", "max"); cp(offG[h], last)
        tt(half(sm), ind(SG, offG[h]), cols(MK, 0, H), "mul")
        act(half(GB), ind(ENT, offG[h]), "id")
        scan(sc, cols(RS0, 0, H), half(sm), 0.0, "mul", "max"); cp(offS[h], last)
        act(half(KN), ind(KW, offS[h]), "id")
        tt(half(dts), ind(DRZ, offS[h]), half(DK), "add"); tt(half(DK), half(dts), half(dtm), "sub")

    kold = new("F", 32); dold = new("B", 32); dlt = new("B", 32); vy = new("F", 32)
    f1 = new("H", 32); r2 = new("I", 32)
    kt = new("F", 32); ky = new("F", 32); dy1 = new("F", 32); dyt = new("F", 32); dy = new("B", 32)
    qy = new("B", 32); sly = new("I", 64); offY = new("U", 32); oky = new("B", 32)
    QS = new("B", 512); AS = new("B", 512); st = new("F", 512); DY = new("B", 512)
    cnt = new("F", W); junk = [new("B", W) for b in range(2)]; acc = new("F", 2)
    lst = [new("U", 2) for s in range(STEPS)]

    def merge(s):
        G, Kp, Z = (cols(rpi[s], 32 * k, 32 * k + 32) for k in range(3))
        ts(f1, Kp, 1024.0, "ge", 1024.0, "mul"); tt(kt, Kp, kold, "max")
        tt(dy1, Z, dold, "add"); tt(dyt, f1, dlt, "mul")
        return G

    def small_look(s):
        L = lst[s - 1]
        G = merge(s - 1)
        tt(ky, kt, f1, "sub"); tt(dy, dy1, dyt, "add")
        wish(SY, 32, G, kt, qy, 2, 3, cols(rpi[s - 1], 96, 128))
        slots(SY, 32, qy, dy, "on", sly, 2, 3)
        cp(offY, cols(sly, 0, 32))
        n = 32 // NQY
        for b in range(NQY):
            x, y = 16 * n * b, 16 * n * (b + 1)
            o = bank(b % 2, 0, y - x)
            act(cols(QS, x, y), ind(qy, cols(REPO, n * b, n * b + n)), "id")
            tt(cols(DY, x, y), ind(TAB, cols(offY, n * b, n * b + n)), cols(QS, x, y), "sub")
            act(cols(AS, x, y), cols(DY, x, y), "abs")
            mm([(o, BN, cols(PT, 0, y - x))], stop=False); mm([(o, BP, cols(AS, x, y))], start=False)
            scan(cols(st, x, y), cols(RS0, 0, y - x), o, 0.0, "mul", "min")
        tt(ind(NF, L), cols(st, 15, 512, 16), vy, "max")
        cp(ind(QB, L), qy); cp(ind(SLN, L), cols(sly, 32, 64))
        o = bank(2, 0, 32)
        mm([(o, cols(UM, 15 - r, 143 - r), cols(AS, r, 512, 16)) for r in range(16)])
        act(oky, o, "sign", thp, -1.0)
        cp(ind(OK, L), oky); cp(ind(SLO, L), cols(sly, 0, 32)); cp(ind(KB, L), ky); cp(ind(DK, L), dy)

    def ask(s):
        scan(cnt, NF, ONEF, 0.0, "add", "add")
        for b in range(2):
            act(junk[b], cnt, "sign", cols(JB, b, b + 1), -1.0, cols(acc, b, b + 1))
        ts(lst[s], acc, 0.5, "mul", W / 2.0, "add")
        cp(cols(asko[s], 32, 64), ind(SLN, lst[s]))
        act(cols(asko[s], 0, 32), ind(QB, lst[s]), "id")
        send("ma%d" % s, asko[s], aski[s], True, HOP2)
        act(kold, ind(KB, lst[s]), "id"); act(dold, ind(DK, lst[s]), "id"); act(vy, ind(VC, lst[s]), "id")
        mm([(bank(3, 0, 32), DM, dold)]); act(dlt, bank(3, 0, 32), "id", 0.0, 1.0 / 1024)

    so = new("U", 32); idx = new("U", 2); sm2 = new("F", 32); sc2 = new("F", 32); of2 = new("U", 2)

    def serve(s):
        q = cols(aski[s], 0, 32)
        cp(so, cols(aski[s], 32, 64))
        n = 32 // NQS
        for b in range(NQS):
            x, y = 16 * n * b, 16 * n * (b + 1)
            o = bank(b % 2, 0, y - x)
            act(cols(QS, x, y), ind(q, cols(REPO, n * b, n * b + n)), "id")
            tt(cols(DW, 32 + x, 32 + y), ind(TAB, cols(so, n * b, n * b + n)), cols(QS, x, y), "sub")
            act(cols(AS, x, y), cols(DW, 32 + x, 32 + y), "abs")
            mm([(o, BP, cols(PT, 0, y - x)), (o, ML, cols(MR2, x % 256, x % 256 + y - x))], stop=False)
            mm([(o, BN, cols(AS, x, y))], start=False)
            scan(cols(st, x, y), o, cols(POS, x, y), cols(st, x - 1, x) if x % 256 else cols(PW, x // 256, x // 256 + 1), "max", "min")
        for b in range(2):
            dst, src = cols(SW, 32 + 256 * b, 288 + 256 * b), ind(SGT, cols(so, 16 * b, 16 * b + 16))
            cp(dst, src) if SGK[b] == "v" else act(dst, src, "id")
        cp(idx, cols(st, 255, 512, 256))
        tt(sm2, ind(SW, idx), cols(MK, 0, 32), "mul")
        tt(cols(rpo[s], 0, 32), ind(DW, idx), q, "add")
        if s < STEPS - 1:
            row_rho(cols(rpo[s], 96, 128), r2, bank(2, 0, 32), 32, cols(rpo[s], 0, 32), B16h)
        scan(sc2, cols(RS0, 0, 32), sm2, 0.0, "mul", "max"); cp(of2, cols(sc2, 15, 32, 16))
        cp(cols(rpo[s], 32, 64), ind(LS, of2)); cp(cols(rpo[s], 64, 96), ind(DRZ, of2))
        send("mr%d" % s, rpo[s], rpi[s], False, HOP2)

    for s in range(STEPS):
        if s == 0:
            tables()
        marks.append(len(ops))
        for h in range(2):
            big_look(h, KINDS if s else KINDS0)
        if s:
            small_look(s)
        ask(s)
        serve(s)
        big_update(0); big_update(1)
    marks.append(len(ops))
    OG = new("F", W); OD = new("F", W); L = lst[STEPS - 1]
    mset(cols(OG, P, W), 0.0); mset(cols(OD, P, W), 0.0)
    act(cols(KB, 0, P), KN, "id"); act(cols(OG, 0, P), GB, "id"); act(cols(OD, 0, P), cols(DK, 0, P), "id")
    G = merge(STEPS - 1)
    cp(ind(OG, L), G); tt(ky, kt, f1, "sub"); cp(ind(KB, L), ky); tt(ind(OD, L), dy1, dyt, "add")

    def store(q, name, a, src):
        add(q, "store", (name, a, src), [src], [], 0.1, 2.2)
    store("s", "yg", None, cols(OG, 0, P)); store("a", "yk", None, cols(KB, 0, P))
    for d in range(4):
        store("sa"[d % 2], "yd", d, rows(cols(OD, 0, P), 12 - 4 * d, 128, 16))
    per = marks[2] - marks[1]
    for i, o in enumerate(ops):
        o["role"] = i if i < marks[2] else (marks[1] + (i - marks[1]) % per if i < marks[-1] else marks[2] + i - marks[-1])
    return ops, top


def depend(ops):
    hist = {}
    for i, o in enumerate(ops):
        d = set()
        spans = []
        for v, wr in [(v, False) for v in o["r"]] + [(v, True) for v in o["w"]]:
            spans.append((v[0], 0, 1, True) if v[0][0] == "P" else (v[0], v[1], v[2], wr))
        for b, x, y, wr in spans:
            for (x2, y2, wr2, j) in hist.get(b, []):
                if x < y2 and x2 < y and (wr or wr2):
                    d.add(j)
        for b, x, y, wr in spans:
            h = hist.setdefault(b, [])
            if wr:
                h[:] = [e for e in h if not (x <= e[0] and e[1] <= y)]
            h.append((x, y, wr, i))
        d.discard(i)
        o["deps"] = d


def schedule(ops, wts=None):
    n = len(ops)
    dur = [o["dur"] for o in ops]
    succ = [[] for i in range(n)]
    for i, o in enumerate(ops):
        es = [(j, ops[j]["lat"] + (0.0 if ops[j]["eng"] is None or ops[j]["eng"] == o["eng"] == "t" else SEM)) for j in o["deps"]]
        if "after" in o:
            es.append(o["after"])
        for j, e in es:
            succ[j].append((i, e))
    lvl = [0.0] * n
    for i in range(n - 1, -1, -1):
        lvl[i] = max([ops[i]["lat"]] + [e + lvl[k] for k, e in succ[i]]) + 1e-6 + (0.1 * wts[ops[i]["role"]] if wts else 0.0)
    busy = {}
    ready = [0.0] * n
    for i in sorted(range(n), key=lambda i: (-lvl[i], i)):
        t = ready[i]
        if ops[i]["eng"] is not None:
            line = busy.setdefault(ops[i]["eng"], [])
            k = len(line)
            while k > 0 and line[k - 1][1] > t:
                k -= 1
            while k < len(line) and t + dur[i] > line[k][0]:
                t = max(t, line[k][1])
                k += 1
            line.insert(k, (t, t + dur[i]))
        ops[i]["t"] = t
        for k2, e in succ[i]:
            ready[k2] = max(ready[k2], t + e + 1e-6)
    return sorted(range(n), key=lambda i: (ops[i]["t"], i))


def needed(ops, order):
    live = set(i for i, o in enumerate(ops) if o["kind"] in ("store", "send", "recv"))
    for i in range(len(ops) - 1, -1, -1):
        if i in live:
            live |= ops[i]["deps"]
    return [i for i in order if i in live]


def syncs(ops, order):
    pos = {}
    known = {}
    for i in order:
        o = ops[i]
        e = o["eng"]
        own = o["kind"] in ("load", "store", "recv")
        o["lane"] = ("x", i) if own else e
        pos[e] = pos.get(e, 0) + 1
        o["pos"] = 1 if own else pos[e]
        o["waits"] = []
        if e is None:
            o["clock"] = {o["lane"]: 1}
            continue
        k = known.setdefault(e, {})
        for j in sorted(o["deps"], key=lambda j: -ops[j]["t"]):
            pj = ops[j]
            if pj["kind"] == "send" or (pj["eng"] == "t" and e == "t"):
                continue
            if k.get(pj["lane"], 0) >= pj["pos"]:
                continue
            o["waits"].append(j)
            pj["sig"] = True
            for l, c in pj["clock"].items():
                if k.get(l, 0) < c:
                    k[l] = c
        c = dict(k)
        c[o["lane"]] = o["pos"]
        o["clock"] = c
    cnt = {}
    for i in order:
        o = ops[i]
        if o["kind"] in ("load", "store"):
            o["sem"] = ("d%d" % len([1 for x in cnt if x[0] == "d"]), 16)
            cnt[o["sem"][0]] = 16
        elif o["kind"] == "recv":
            o["sem"] = (o["args"][0], None)
        elif o.get("sig"):
            nm_ = "q" + o["eng"]
            cnt[nm_] = cnt.get(nm_, 0) + 1
            o["sem"] = (nm_, cnt[nm_])
    return cnt


OPS, TOP = build()
depend(OPS)
ORDER = needed(OPS, schedule(OPS, [VAL[c] for c in PRIO]))
FINAL = syncs(OPS, ORDER)
MSGS = [OPS[i]["args"] for i in ORDER if OPS[i]["kind"] == "send"]

SCRATCH = {"sb" + k: ("sbuf", [128, TOP[k]], DTYPE[k]) for k in SIZE}
SCRATCH.update({"ps%d" % i: ("psum", [128, 512], "float32") for i in range(8)})
SEMAPHORES = sorted(FINAL) + [m[0] for m in MSGS] + ["sent"]


def count(mask):
    return bin(mask).count("1")


def relay_of(T, topo, rank):
    n = len(T.cores)
    c = T.cores[rank]
    ok = [x for x in topo.cores_of(c) if x not in T.cores and topo.may_write(x, T.cores[(rank + 1) % n])
          and topo.may_write(x, T.cores[(rank - 1) % n])]
    return sorted(ok, key=lambda x: topo.die(x) != topo.die(c))[0]


def rank_program(g, core, T, topo):
    n = len(T.cores)

    def ap(v):
        if not isinstance(v, tuple):
            return v
        if v[0] == "ind":
            return ap(v[1]).indirect(ap(v[2]))
        t = T["ps" + v[0][1:]] if v[0][0] == "P" else T["sb" + v[0]]
        if v[6] != 1:
            return t[v[4]:v[5]:v[6], v[1]:v[2]]
        if v[3] != 1:
            return t[v[4]:v[5], v[1]:v[2]:v[3]]
        return t[v[4]:v[5], v[1]:v[2]]

    rank = T.rank_of(core)
    if rank is None:
        for r in range(n):
            if relay_of(T, topo, r) != core:
                continue
            total = 0
            for name, src, dst, nxt in MSGS:
                to = T.cores[(r + (1 if nxt else -1)) % n]
                rid, pid = topo.addr(to, core)
                m = topo.mask(core, to)
                g.wait_ge(T.sem[name], count(topo.mask(T.cores[r], core)))
                g.remote_dma(ap(dst), ap(dst), T.sem[name], T.sem.sent, pid, rid, m)
                total += count(m)
            g.wait_ge(T.sem.sent, total)
        return
    relay = relay_of(T, topo, rank)
    rid, pid = topo.addr(relay, core)
    m1 = topo.mask(core, relay)
    got = {}
    for name, src, dst, nxt in MSGS:
        got[name] = count(topo.mask(relay_of(T, topo, (rank + (-1 if nxt else 1)) % n), core))
    Q = {"g": g, "v": g.vector, "a": g.scalar, "t": g.tensor, "s": g.sync}
    for i in ORDER:
        o = OPS[i]
        k, a = o["kind"], o["args"]
        if k == "recv":
            continue
        q = Q[o["eng"]]
        for j in o["waits"]:
            s, c = OPS[j]["sem"]
            q.wait_ge(T.sem[s], got[s] if c is None else c)
        if k == "send":
            g.remote_dma(ap(a[2]), ap(a[1]), T.sem[a[0]], T.sem.sent, pid, rid, m1)
            continue
        if k == "cp":
            x = q.tensor_copy(ap(a[0]), ap(a[1]))
        elif k == "tt":
            x = q.tensor_tensor(ap(a[0]), ap(a[1]), ap(a[2]), ALU[a[3]])
        elif k == "ts":
            if a[5] is None:
                x = q.tensor_scalar(ap(a[0]), ap(a[1]), ap(a[2]), None, ALU[a[4]])
            else:
                x = q.tensor_scalar(ap(a[0]), ap(a[1]), ap(a[2]), ap(a[3]), ALU[a[4]], ALU[a[5]])
        elif k == "scan":
            x = q.tensor_tensor_scan(ap(a[0]), ap(a[1]), ap(a[2]), ap(a[3]), ALU[a[4]], ALU[a[5]])
        elif k == "mset":
            x = q.memset(ap(a[0]), a[1])
        elif k == "act":
            x = q.activation(ap(a[0]), ap(a[1]), ACT[a[2]], bias=ap(a[3]), scale=ap(a[4]), accum_out=ap(a[5]))
        elif k == "mm":
            for (out, l, r, st, sp) in a:
                x = q.matmul(ap(out), ap(l), ap(r), st, sp)
        elif k == "iota":
            x = g.iota(ap(a[0]), a[1], a[2], a[3], allow_small_or_imprecise_dtypes=True)
        elif k == "asel":
            x = g.affine_select(ap(a[0]), ap(a[1]), a[2], ALU[a[3]], a[4], a[5], a[6])
        elif k == "load":
            x = q.dma_start(ap(a[0]), T[a[1]][:])
        elif k == "store":
            dst = T[a[0]][:] if a[1] is None else T[a[0]][:, a[1] * P:(a[1] + 1) * P]
            x = q.dma_start(dst, ap(a[2]))
        if "sem" in o:
            x.then_inc(T.sem[o["sem"][0]], 16 if k in ("load", "store") else 1)
    for s in sorted(FINAL):
        g.wait_ge(T.sem[s], FINAL[s])
    g.wait_ge(T.sem.sent, len(MSGS) * count(m1))
